import numpy as np
import ml_dtypes


def mxq(x, axis, fmt="e4m3"):
    dtype, down = {"e4m3": (ml_dtypes.float8_e4m3fn, 7), "e5m2": (ml_dtypes.float8_e5m2, 14)}[fmt]
    v = np.moveaxis(np.asarray(x, np.float32).astype(ml_dtypes.bfloat16).astype(np.float64), axis, -1)
    blocks = v.reshape(v.shape[:-1] + (-1, 32))
    amax = np.abs(blocks).max(-1, keepdims=True)
    byte = np.maximum(np.where(amax > 0, np.frexp(amax)[1] - 1 + 127, 0) - down, 1)
    scale = np.exp2(byte - 127.0)
    codes = (blocks / scale).astype(np.float32).astype(dtype).astype(np.float64)
    return np.moveaxis((codes * scale).reshape(v.shape), -1, axis)


WIDE = False


def mx_kscale(k):
    if not WIDE:
        return np.ones(k)
    levels = np.array([10, -10, 5, -5, 0])
    if k % 512:
        return np.exp2(np.random.permutation(np.resize(levels, k // 32))).repeat(32)
    a = np.empty((k // 512, 16))
    for p in range(k // 512):
        a[p, :8] = np.random.permutation(np.resize(levels, 8))
        for g in range(8):
            far = levels[np.abs(levels - a[p, g]) >= 10]
            a[p, g + 8] = far[np.random.randint(len(far))]
    return np.exp2(a.ravel()).repeat(32)


BF16 = ml_dtypes.bfloat16


def bf(x):
    return np.asarray(x, np.float32).astype(BF16)


def f64(x):
    return np.asarray(x).astype(np.float64)


E2M1 = np.array([0.0, 0.5, 1.0, 1.5, 2.0, 3.0, 4.0, 6.0, -0.0, -0.5, -1.0, -1.5, -2.0, -3.0, -4.0, -6.0])


def pack_weight(w, fmt):
    k, n = w.shape
    w = f64(bf(w)).reshape(k // 32, 32, n)
    amax = np.abs(w).max(1)
    if fmt == "e4m3":
        byte = np.frexp(amax)[1] - 1 + 127 - 7
    else:
        mant, ex = np.frexp(amax / 6.0)
        byte = np.where(mant > 0.5, ex, ex - 1) + 127
    byte = np.clip(np.where(amax > 0, byte, 1), 1, 254)
    scaled = (w * np.exp2(127.0 - byte)[:, None, :]).reshape(k, n).astype(np.float32)
    by_word = np.ascontiguousarray(scaled.reshape(k // 512, 128, 4, n).transpose(0, 1, 3, 2))
    if fmt == "e4m3":
        words = by_word.astype(ml_dtypes.float8_e4m3fn).view(np.uint8)
    else:
        c = by_word.astype(ml_dtypes.float4_e2m1fn).view(np.uint8) & 0xF
        words = c[..., 0::2] | (c[..., 1::2] << 4)
    return np.ascontiguousarray(words), np.ascontiguousarray(byte.astype(np.uint8).reshape(k // 512, 16, n))


def unpack_weight(words, scales, fmt):
    g, p, n, _ = words.shape
    if fmt == "e4m3":
        vals = np.ascontiguousarray(words).view(ml_dtypes.float8_e4m3fn).astype(np.float64)
    else:
        nib = np.empty((g, p, n, 4), np.uint8)
        nib[..., 0::2] = words & 0xF
        nib[..., 1::2] = words >> 4
        vals = E2M1[nib]
    vals = vals * np.repeat(np.exp2(scales.astype(np.float64) - 127.0), 8, axis=1)[..., None]
    return vals.transpose(0, 1, 3, 2).reshape(g * 512, n)
def pack4(w):
    words, scales = pack_weight(w, "e2m1")
    return words.reshape(words.shape[0], 128, -1), scales


def unpack4(words, scales):
    return unpack_weight(words.reshape(words.shape[0], 128, -1, 2), scales, "e2m1")


def planes(Y):
    n, m = Y.shape
    b = f64(bf(Y)).reshape(n // 32, 32, m)
    amax = np.abs(b).max(1)
    byte = np.clip(np.where(amax > 0, np.frexp(amax)[1] - 1 + 127 - 7, 1), 1, 254)
    codes = (b * np.exp2(127.0 - byte)[:, None, :]).reshape(n, m).astype(np.float32).astype(ml_dtypes.float8_e4m3fn).view(np.uint8)
    words = codes.reshape(n // 512, 128, 4, m).transpose(0, 1, 3, 2)
    return np.ascontiguousarray(words), np.ascontiguousarray(byte.astype(np.uint8).reshape(n // 512, 16, m))


Q, N, D, T = 1024, 1024, 512, 1024

LOG_AMPLITUDE = 8.4
DIST_SCALE = 128.0

XS = np.sqrt(4.0 * DIST_SCALE / D)


def setup_inputs():
    s, t = mx_kscale(D), mx_kscale(N)
    x = bf(np.random.standard_normal((Q, D)) * XS * s)
    zt = bf(np.random.standard_normal((N, D)) * XS / s)
    lam = bf(np.random.uniform(0.5, 1.5, D) / (s * s))
    c = bf(np.random.standard_normal(N) * t)
    alpha_words, alpha_scales = pack4(np.random.standard_normal((N, T)) / np.sqrt(N) / t[:, None])
    beta_words, beta_scales = pack4(np.random.standard_normal((D, T)) / (XS * np.sqrt(D)) / s[:, None])
    return {"x": x, "zt": zt, "lam": lam, "c": c, "alpha_words": alpha_words, "alpha_scales": alpha_scales, "beta_words": beta_words, "beta_scales": beta_scales}


def core(x, zt, lam, c, alpha_words, alpha_scales, beta_words, beta_scales):
    x, zt, lam, c = f64(x), f64(zt), f64(lam), f64(c)
    nx = np.sum(lam[None, :] * np.square(x), axis=1)
    nz = np.sum(np.square(zt) / lam[None, :], axis=1)
    xq = mxq(x, 1, "e4m3")
    dot = xq @ mxq(zt, 1, "e4m3").T
    k = np.exp(LOG_AMPLITUDE - (nx[:, None] + nz[None, :] - 2.0 * dot) / DIST_SCALE)
    kc = k * c[None, :]
    lin = xq @ unpack4(beta_words, beta_scales)
    return lin + (mxq(kc, 1, "e4m3") @ unpack4(alpha_words, alpha_scales))


def reference(x, zt, lam, c, alpha_words, alpha_scales, beta_words, beta_scales):
    R_out = core(x, zt, lam, c, alpha_words, alpha_scales, beta_words, beta_scales)
    words, scales = planes(R_out.T)
    return R_out, words, scales

@@ -1,0 +1,477 @@
+from contextlib import ExitStack
+
+import concourse.mybir as mybir
+from concourse.masks import make_identity
+
+Q, N, D, T = 1024, 1024, 512, 1024
+FLOPS = 2 * (Q * N * D + Q * D * T + Q * N * T)
+
+F32 = mybir.dt.float32
+BF16 = mybir.dt.bfloat16
+U32 = mybir.dt.uint32
+I32 = mybir.dt.int32
+U8 = mybir.dt.uint8
+FP8X4 = mybir.dt.float8_e4m3fn_x4
+FP4X4 = mybir.dt.float4_e2m1fn_x4
+ALU = mybir.AluOpType
+ACT = mybir.ActivationFunctionType
+
+P = 128
+LOG_AMPLITUDE = 8.4
+DIST_SCALE = 128.0
+
+
+def tile_ardgaussianprocessmean_x2_kernel(
+    tc, x, zt, lam, c, alpha_words, alpha_scales, beta_words, beta_scales, out_0, out_1, out_2
+):
+    nc = tc.nc
+    with ExitStack() as ctx:
+        keep = ctx.enter_context(tc.tile_pool(name="keep", bufs=1))
+        work = ctx.enter_context(tc.tile_pool(name="work", bufs=2))
+        psum_t = ctx.enter_context(tc.psum_pool(name="psum_t", bufs=2))
+        psum_1 = ctx.enter_context(tc.psum_pool(name="psum_1", bufs=2))
+        psum_2 = ctx.enter_context(tc.psum_pool(name="psum_2", bufs=3))
+        psum_n = ctx.enter_context(tc.psum_pool(name="psum_n", bufs=1))
+        ctx.enter_context(tc.manual_schedule())
+
+        lam_col = keep.tile([P, 4], BF16)
+        nc.scalar.dma_start(out=lam_col[:], in_=lam.rearrange("(p t) -> p t", t=4))
+        c_col = keep.tile([P, 2, 4], BF16)
+        nc.scalar.dma_start(out=c_col[:], in_=c.rearrange("(g m t) -> m g t", g=2, t=4))
+
+        z_raw = keep.tile([P, 2, 4, D], BF16, align_bytes=64)
+        x_raw = keep.tile([P, 8, D], BF16, align_bytes=64)
+
+        def load_z(g, a):
+            nc.sync.dma_start(
+                out=z_raw[:, g, 2 * a : 2 * a + 2, :],
+                in_=zt[512 * g : 512 * g + 512, :].rearrange("(m t) d -> m t d", t=4)[:, 2 * a : 2 * a + 2, :],
+            )
+
+        def load_x(i0, n):
+            nc.sync.dma_start(
+                out=x_raw[:, i0 : i0 + n, :],
+                in_=x[128 * i0 : 128 * (i0 + n), :].rearrange("(i m) d -> m i d", m=P),
+            )
+
+        load_z(0, 0)
+        load_z(0, 1)
+        load_x(0, 2)
+        load_z(1, 0)
+        load_z(1, 1)
+        load_x(2, 2)
+        load_x(4, 2)
+        load_x(6, 2)
+
+        w_scales = keep.tile([P, 3, T], U8, align_bytes=64)
+        nc.vector.memset(w_scales[:].bitcast(I32), 0)
+        w_words = keep.tile([P, 3, 2 * T], U8, align_bytes=64)
+        nc.sync.dma_start(out=w_words[:, 0, :].bitcast(I32), in_=beta_words[0].bitcast(I32))
+        for g in range(2):
+            nc.sync.dma_start(out=w_words[:, 1 + g, :].bitcast(I32), in_=alpha_words[g].bitcast(I32))
+        for k in range(4):
+            rows = slice(4 * k, 4 * k + 4)
+            parts = slice(32 * k, 32 * k + 4)
+            nc.sync.dma_start(
+                out=w_scales[parts, 0:1, :].bitcast(I32),
+                in_=beta_scales[:, rows, :].rearrange("g q n -> q g n").bitcast(I32),
+            )
+            nc.sync.dma_start(
+                out=w_scales[parts, 1:3, :].bitcast(I32),
+                in_=alpha_scales[:, rows, :].rearrange("g q n -> q g n").bitcast(I32),
+            )
+
+        ident = keep.tile([P, P], F32)
+        make_identity(nc, ident[:])
+
+        lam_f = keep.tile([P, 4], F32)
+        nc.vector.tensor_copy(out=lam_f[:], in_=lam_col[:])
+        lam_inv = keep.tile([P, 4], F32)
+        nc.vector.reciprocal(out=lam_inv[:], in_=lam_f[:])
+
+        lam_half = keep.tile([P, 4], F32)
+        nc.vector.tensor_scalar(out=lam_half[:], in0=lam_col[:], scalar1=0.5, scalar2=None, op0=ALU.mult)
+        halves = keep.tile([P, 4], F32)
+        nc.gpsimd.memset(halves[:], 0.5)
+        root = keep.tile([P, 4], F32)
+        nc.gpsimd.tensor_tensor(out=root[:], in0=lam_half[:], in1=halves[:], op=ALU.pow)
+        c_flat = c_col[:].rearrange("p g t -> p (g t)")
+        c_abs = keep.tile([P, 8], F32)
+        nc.vector.scalar_tensor_tensor(out=c_abs[:], in0=c_flat, scalar=-1.0, in1=c_flat, op0=ALU.mult, op1=ALU.max)
+        c_neg = keep.tile([P, 8], BF16)
+        nc.vector.tensor_scalar(out=c_neg[:], in0=c_flat, scalar1=0.0, scalar2=None, op0=ALU.is_lt)
+        nc.vector.tensor_scalar_max(out=c_abs[:], in0=c_abs[:], scalar1=1.2e-38)
+        c_sign = keep.tile([P, 2, 4], BF16)
+        nc.vector.scalar_tensor_tensor(
+            out=c_sign[:].rearrange("p g t -> p (g t)"), in0=c_flat, scalar=0.0, in1=c_neg[:], op0=ALU.is_gt, op1=ALU.subtract
+        )
+        c_log = keep.tile([P, 8], F32)
+        nc.scalar.activation(out=c_log[:], in_=c_abs[:], func=ACT.Ln)
+        warm = keep.tile([P, 1], F32)
+        nc.scalar.activation(out=warm[:], in_=c_log[:, 0:1], func=ACT.Exp)
+        c_off = keep.tile([P, 8], F32)
+        nc.vector.tensor_scalar(
+            out=c_off[:], in0=c_log[:], scalar1=DIST_SCALE / 2, scalar2=LOG_AMPLITUDE * DIST_SCALE / 2,
+            op0=ALU.mult, op1=ALU.add,
+        )
+
+        z_grp = keep.tile([P, N, 4], BF16, align_bytes=64)
+        x_grp = keep.tile([P, Q, 4], BF16, align_bytes=64)
+        z_codes = keep.tile([P, N], U32, align_bytes=64)
+        z_scales = keep.tile([P, N], U8, align_bytes=64)
+        x_codes = keep.tile([P, Q], U32, align_bytes=64)
+        x_scales = keep.tile([P, Q], U8, align_bytes=64)
+        norm_ps = psum_n.tile([P, 16], F32)
+        z_bias = keep.tile([P, 8], F32)
+        nx_half = keep.tile([P, 8], F32)
+        nx_row = keep.tile([P, Q], F32)
+
+        copy_on = {"V": nc.vector.tensor_copy, "S": nc.scalar.copy}
+
+        turned = {}
+
+        def turn_pair(name, raw):
+            tp = psum_t.tile([P, 2, 2, P], F32, tag="tp")
+            for a in range(2):
+                words = raw[:, a, :].bitcast(F32)
+                for u in range(2):
+                    nc.tensor.transpose(tp[:, a, u, :], words[:, u : 256 : 2], ident[:])
+            turned[name] = tp
+
+        def pair_copy(name, grp, on):
+            tp = turned[name]
+            copy_on[on](
+                out=grp.bitcast(F32).rearrange("p (a r) u -> p a r u", a=2),
+                in_=tp[:].rearrange("p a u r -> p a r u"),
+            )
+
+        def quant(grp, codes, scales):
+            nc.vector.quantize_mx(
+                out=codes.bitcast(FP8X4), scales=scales, in_=grp.rearrange("p r t -> p (r t)")
+            )
+
+        def z_turn(k):
+            turn_pair(("z", k), z_raw[:, k // 2, 2 * (k % 2) : 2 * (k % 2) + 2, :])
+
+        def z_copy(k, on):
+            pair_copy(("z", k), z_grp[:, 256 * k : 256 * k + 256, :], on)
+
+        def x_turn(k):
+            turn_pair(("x", k), x_raw[:, 2 * k : 2 * k + 2, :])
+
+        def x_copy(k, on):
+            pair_copy(("x", k), x_grp[:, 256 * k : 256 * k + 256, :], on)
+
+        def z_quant(c0, c1):
+            quant(z_grp[:, c0:c1, :], z_codes[:, c0:c1], z_scales[:, c0:c1])
+
+        def x_quant(c0, c1):
+            quant(x_grp[:, c0:c1, :], x_codes[:, c0:c1], x_scales[:, c0:c1])
+
+        spreads = {}
+        root_row = keep.tile([P, D], F32)
+
+        def root_spread():
+            sp = psum_t.tile([P, 4, P], F32, tag="tp")
+            for t in range(4):
+                nc.tensor.matmul(
+                    out=sp[:, t, :], lhsT=root[:, t : t + 1].to_broadcast([P, P]), rhs=ident[:], start=True, stop=True
+                )
+            spreads["root"] = sp
+
+        def root_copy():
+            sp = spreads["root"]
+            nc.scalar.copy(out=root_row[:].rearrange("m (p t) -> m p t", t=4), in_=sp[:].rearrange("m t p -> m p t"))
+
+        def x_scaled(i):
+            y = work.tile([P, D], F32, tag="xl", bufs=3)
+            squares["row", i] = y
+            nc.gpsimd.tensor_tensor(out=y[:], in0=x_raw[:, i, :], in1=root_row[:], op=ALU.mult)
+
+        def x_norm(i):
+            junk = work.tile([P, D], F32, tag="junk", bufs=2)
+            nc.scalar.activation(out=junk[:], in_=squares["row", i][:], func=ACT.Square, accum_out=nx_half[:, i : i + 1])
+
+        squares = {}
+
+        def square(which, k, on):
+            grp = (z_grp if which == "z" else x_grp)[:, 256 * k : 256 * k + 256, :].rearrange("p r t -> p t r")
+            sq = work.tile([P, 4, 256], F32, tag="sq", bufs=4)
+            squares[which, k] = sq
+            if on == "S":
+                nc.scalar.activation(out=sq[:], in_=grp, func=ACT.Square)
+            else:
+                nc.gpsimd.tensor_tensor(out=sq[:], in0=grp, in1=grp, op=ALU.mult)
+
+        def norm_sum(which, k):
+            sq = squares[which, k]
+            for b in range(2):
+                col = 2 * k + b + (0 if which == "z" else 8)
+                for t in range(4):
+                    nc.tensor.matmul(
+                        out=norm_ps[:, col : col + 1],
+                        lhsT=sq[:, t, P * b : P * b + P],
+                        rhs=(lam_inv if which == "z" else lam_f)[:, t : t + 1],
+                        start=(t == 0),
+                        stop=(t == 3),
+                    )
+
+        def z_bias_of(g):
+            gc = slice(4 * g, 4 * g + 4)
+            nc.vector.scalar_tensor_tensor(
+                out=z_bias[:, gc], in0=norm_ps[:, gc], scalar=-0.5, in1=c_off[:, gc], op0=ALU.mult, op1=ALU.add
+            )
+
+        def x_half_of(k):
+            nc.vector.tensor_scalar(
+                out=nx_half[:, 2 * k : 2 * k + 2], in0=norm_ps[:, 8 + 2 * k : 10 + 2 * k], scalar1=0.5, scalar2=None, op0=ALU.mult
+            )
+
+        def x_spread(k):
+            sp = psum_t.tile([P, 2, P], F32, tag="tp")
+            for b in range(2):
+                i = 2 * k + b
+                nc.tensor.matmul(
+                    out=sp[:, b, :], lhsT=nx_half[:, i : i + 1].to_broadcast([P, P]), rhs=ident[:], start=True, stop=True
+                )
+            spreads[k] = sp
+
+        def x_spread_copy(k, on):
+            sp = spreads[k]
+            copy_on[on](out=nx_row[:, 256 * k : 256 * k + 256], in_=sp[:].rearrange("p k m -> p (k m)"))
+
+        k_codes = keep.tile([P, 4, 2, 256], U32, align_bytes=64)
+        k_scales = keep.tile([P, 4, 2, 256], U8, align_bytes=64)
+        args = {}
+        exps = {}
+
+        scs = {}
+
+        def score_mm(k, g, tt):
+            cols = slice(256 * k, 256 * k + 256)
+            ps = psum_1.tile([P, 2, 256], F32, tag="ps1")
+            scs[k, g, tt] = ps
+            for b in range(2):
+                j = 4 * g + 2 * tt + b
+                nc.tensor.matmul_mx(
+                    out=ps[:, b, :],
+                    lhsT=z_codes[:, P * j : P * j + P].bitcast(FP8X4),
+                    lhsT_scale=z_scales[:, P * j : P * j + P],
+                    rhs=x_codes[:, cols].bitcast(FP8X4),
+                    rhs_scale=x_scales[:, cols],
+                    start=True,
+                    stop=True,
+                )
+
+        def score_add(k, g, tt):
+            cols = slice(256 * k, 256 * k + 256)
+            if tt == 0:
+                args[k, g] = work.tile([P, 4, 256], F32, tag="arg", bufs=4, name="arg")
+            arg = args[k, g]
+            ps = scs[k, g, tt]
+            for b in range(2):
+                j = 4 * g + 2 * tt + b
+                nc.vector.scalar_tensor_tensor(
+                    out=arg[:, 2 * tt + b, :], in0=ps[:, b, :], scalar=z_bias[:, j : j + 1], in1=nx_row[:, cols],
+                    op0=ALU.add, op1=ALU.subtract,
+                )
+
+        def expo(k, g):
+            if g == 0:
+                exps[k] = work.tile([P, 2, 256, 4], BF16, tag="ex", bufs=3, align_bytes=64, name="ex")
+            nc.scalar.activation(
+                out=exps[k][:, g, :, :], in_=args[k, g][:].rearrange("p t q -> p q t"), func=ACT.Exp, scale=2.0 / DIST_SCALE
+            )
+
+        def sign(k, g):
+            ex = exps[k][:, g, :, :]
+            nc.vector.tensor_tensor(out=ex, in0=ex, in1=c_sign[:, g : g + 1, :].to_broadcast([P, 256, 4]), op=ALU.mult)
+
+        def k_quant(k):
+            nc.vector.quantize_mx(
+                out=k_codes[:, k, :, :].rearrange("p g q -> p (g q)").bitcast(FP8X4),
+                scales=k_scales[:, k, :, :].rearrange("p g q -> p (g q)"),
+                in_=exps[k][:].rearrange("p g q t -> p (g q t)"),
+            )
+
+        rs = {}
+        rbs = {}
+        ps2s = {}
+        tps = {}
+        ys = {}
+
+        def product(i, g):
+            cols = slice(P * i, P * i + P)
+            if g == 0:
+                rs[i] = work.tile([P, T], F32, tag="r", bufs=5, name="r")
+                rbs[i] = work.tile([P, 2, 2, P, 2], BF16, tag="rb", bufs=3, align_bytes=64, name="rb")
+            ps = psum_2.tile([P, 512], F32, tag="ps2")
+            ps2s[i, g] = ps
+            kq = slice(P * (i % 2), P * (i % 2) + P)
+            for k in range(3):
+                nc.tensor.matmul_mx(
+                    out=ps[:],
+                    lhsT=(x_codes[:, cols] if k == 0 else k_codes[:, i // 2, k - 1, kq]).bitcast(FP8X4),
+                    lhsT_scale=x_scales[:, cols] if k == 0 else k_scales[:, i // 2, k - 1, kq],
+                    rhs=w_words[:, k, 1024 * g : 1024 * g + 1024].bitcast(FP4X4),
+                    rhs_scale=w_scales[:, k, 512 * g : 512 * g + 512],
+                    start=(k == 0),
+                    stop=(k == 2),
+                )
+
+        def r_out(i, g):
+            nc.scalar.copy(out=rs[i][:, 512 * g : 512 * g + 512], in_=ps2s[i, g][:])
+            if g == 1:
+                nc.sync.dma_start(out=out_0[P * i : P * i + P, :], in_=rs[i][:])
+
+        def r_round(i, g):
+            nc.vector.tensor_copy(
+                out=rbs[i][:, g, :, :, :],
+                in_=rs[i][:, 512 * g : 512 * g + 512].rearrange("q (p u e) -> q u p e", u=2, e=2),
+            )
+
+        def r_turn(i, g):
+            if g == 0:
+                tps[i] = psum_t.tile([P, 2, 2, P], F32, tag="tp", name="tp")
+            for u in range(2):
+                nc.tensor.transpose(
+                    tps[i][:, g, u, :], rbs[i][:, g, u, :, :].rearrange("q p e -> q (p e)").bitcast(F32), ident[:]
+                )
+
+        def y_copy(i, on):
+            if i % 2 == 0:
+                ys[i // 2] = work.tile([P, 2, 256, 4], BF16, tag="y_grp", bufs=3, align_bytes=64, name="y_grp")
+            a = i % 2
+            copy_on[on](
+                out=ys[i // 2][:, :, P * a : P * a + P, :].bitcast(F32), in_=tps[i][:].rearrange("p g u r -> p g r u")
+            )
+
+        def y_quant(k):
+            y_codes = work.tile([P, 2, 256], U32, tag="y_codes", bufs=4, align_bytes=64)
+            y_scales = work.tile([P, 2, 256], U8, tag="y_scales", bufs=4, align_bytes=64)
+            nc.vector.quantize_mx(
+                out=y_codes[:].rearrange("p g r -> p (g r)").bitcast(FP8X4),
+                scales=y_scales[:].rearrange("p g r -> p (g r)"),
+                in_=ys[k][:].rearrange("p g r t -> p (g r t)"),
+            )
+            q0 = 256 * k
+            nc.sync.dma_start(
+                out=out_1[:, :, q0 : q0 + 256, :].rearrange("g p m t -> p g (m t)").bitcast(I32),
+                in_=y_codes[:].bitcast(I32),
+            )
+            for b in range(4):
+                nc.sync.dma_start(
+                    out=out_2[:, 4 * b : 4 * b + 4, q0 : q0 + 256].rearrange("g q n -> q g n").bitcast(I32),
+                    in_=y_scales[32 * b : 32 * b + 4, :, :].bitcast(I32),
+                )
+
+        z_turn(0)
+        z_turn(1)
+        root_spread()
+        root_copy()
+        z_copy(0, "V")
+        square("z", 0, "S")
+        z_copy(1, "V")
+        square("z", 1, "S")
+        x_turn(0)
+        x_copy(0, "V")
+        z_quant(0, 512)
+        x_scaled(0)
+        x_scaled(1)
+        norm_sum("z", 0)
+        norm_sum("z", 1)
+        z_bias_of(0)
+        x_quant(0, 256)
+        x_norm(0)
+        x_norm(1)
+        z_turn(2)
+        z_copy(2, "V")
+        square("z", 2, "S")
+        x_spread(0)
+        x_spread_copy(0, "S")
+        score_mm(0, 0, 0)
+        score_mm(0, 0, 1)
+        z_turn(3)
+        z_copy(3, "V")
+        square("z", 3, "S")
+        score_add(0, 0, 0)
+        score_add(0, 0, 1)
+        x_scaled(2)
+        x_scaled(3)
+        norm_sum("z", 2)
+        x_turn(1)
+        z_quant(512, 1024)
+        expo(0, 0)
+        norm_sum("z", 3)
+        z_bias_of(1)
+        x_copy(1, "S")
+        x_norm(2)
+        x_norm(3)
+        x_quant(256, 512)
+        score_mm(0, 1, 0)
+        score_mm(0, 1, 1)
+        x_spread(1)
+        x_spread_copy(1, "S")
+        score_add(0, 1, 0)
+        score_add(0, 1, 1)
+        x_turn(2)
+        x_copy(2, "S")
+        square("x", 2, "G")
+        score_mm(1, 0, 0)
+        score_mm(1, 0, 1)
+        expo(0, 1)
+        x_turn(3)
+        x_copy(3, "S")
+        square("x", 3, "G")
+        sign(0, 0)
+        score_add(1, 0, 0)
+        score_add(1, 0, 1)
+        x_quant(512, 1024)
+        score_mm(1, 1, 0)
+        score_mm(1, 1, 1)
+        expo(1, 0)
+        sign(0, 1)
+        k_quant(0)
+        norm_sum("x", 2)
+        x_half_of(2)
+        x_spread(2)
+        x_spread_copy(2, "S")
+        score_add(1, 1, 0)
+        score_add(1, 1, 1)
+        for j in range(3, 13):
+            i = j - 3
+            if i < 8:
+                product(i, 0)
+            h = j + 1
+            if h < 8:
+                score_mm(h // 2, h % 2, 0)
+                score_mm(h // 2, h % 2, 1)
+            if 3 <= h + 0 and h - 1 < 8:
+                expo((h - 1) // 2, (h - 1) % 2)
+            if i < 8:
+                r_out(i, 0)
+                product(i, 1)
+            if h < 8:
+                score_add(h // 2, h % 2, 0)
+            if h - 2 < 8:
+                sign((h - 2) // 2, (h - 2) % 2)
+                if (h - 2) % 2 == 1:
+                    k_quant((h - 2) // 2)
+            if i < 8:
+                r_round(i, 0)
+            if h < 8:
+                score_add(h // 2, h % 2, 1)
+            if i < 8:
+                r_out(i, 1)
+                r_round(i, 1)
+            if j == 3:
+                norm_sum("x", 3)
+                x_half_of(3)
+                x_spread(3)
+                x_spread_copy(3, "S")
+            if 1 <= i < 9:
+                r_turn(i - 1, 0)
+                r_turn(i - 1, 1)
+                y_copy(i - 1, "SSSSVVVV"[i - 1])
+            if i >= 2 and i % 2 == 0:
+                y_quant(i // 2 - 1)

@@ -29,15 +29,14 @@ def tile_ardgaussianprocessmean_x2_kernel(
         keep = ctx.enter_context(tc.tile_pool(name="keep", bufs=1))
         work = ctx.enter_context(tc.tile_pool(name="work", bufs=2))
         psum_t = ctx.enter_context(tc.psum_pool(name="psum_t", bufs=2))
-        psum_1 = ctx.enter_context(tc.psum_pool(name="psum_1", bufs=2))
+        psum_1 = ctx.enter_context(tc.psum_pool(name="psum_1", bufs=3))
         psum_2 = ctx.enter_context(tc.psum_pool(name="psum_2", bufs=3))
-        psum_n = ctx.enter_context(tc.psum_pool(name="psum_n", bufs=1))
         ctx.enter_context(tc.manual_schedule())
 
         lam_col = keep.tile([P, 4], BF16)
-        nc.scalar.dma_start(out=lam_col[:], in_=lam.rearrange("(p t) -> p t", t=4))
         c_col = keep.tile([P, 2, 4], BF16)
         nc.scalar.dma_start(out=c_col[:], in_=c.rearrange("(g m t) -> m g t", g=2, t=4))
+        nc.scalar.dma_start(out=lam_col[:], in_=lam.rearrange("(p t) -> p t", t=4))
 
         z_raw = keep.tile([P, 2, 4, D], BF16, align_bytes=64)
         x_raw = keep.tile([P, 8, D], BF16, align_bytes=64)
@@ -64,11 +63,21 @@ def tile_ardgaussianprocessmean_x2_kernel(
         load_x(6, 2)
 
         w_scales = keep.tile([P, 3, T], U8, align_bytes=64)
-        nc.vector.memset(w_scales[:].bitcast(I32), 0)
         w_words = keep.tile([P, 3, 2 * T], U8, align_bytes=64)
         nc.sync.dma_start(out=w_words[:, 0, :].bitcast(I32), in_=beta_words[0].bitcast(I32))
         for g in range(2):
             nc.sync.dma_start(out=w_words[:, 1 + g, :].bitcast(I32), in_=alpha_words[g].bitcast(I32))
+
+        one = keep.tile([P, 1], F32)
+        nc.vector.memset(one[:], 1.0)
+        halves = keep.tile([P, 8], F32)
+        nc.vector.memset(halves[:], 0.5)
+        warm = keep.tile([P, 2], F32)
+        nc.scalar.activation(out=warm[:, 0:1], in_=one[:], func=ACT.Ln)
+        ident = keep.tile([P, P], F32)
+        make_identity(nc, ident[:])
+
+        nc.vector.memset(w_scales[:].bitcast(I32), 0)
         for k in range(4):
             rows = slice(4 * k, 4 * k + 4)
             parts = slice(32 * k, 32 * k + 4)
@@ -81,39 +90,34 @@ def tile_ardgaussianprocessmean_x2_kernel(
                 in_=alpha_scales[:, rows, :].rearrange("g q n -> q g n").bitcast(I32),
             )
 
-        ident = keep.tile([P, P], F32)
-        make_identity(nc, ident[:])
-
-        lam_f = keep.tile([P, 4], F32)
-        nc.vector.tensor_copy(out=lam_f[:], in_=lam_col[:])
-        lam_inv = keep.tile([P, 4], F32)
-        nc.vector.reciprocal(out=lam_inv[:], in_=lam_f[:])
-
-        lam_half = keep.tile([P, 4], F32)
-        nc.vector.tensor_scalar(out=lam_half[:], in0=lam_col[:], scalar1=0.5, scalar2=None, op0=ALU.mult)
-        halves = keep.tile([P, 4], F32)
-        nc.gpsimd.memset(halves[:], 0.5)
-        root = keep.tile([P, 4], F32)
-        nc.gpsimd.tensor_tensor(out=root[:], in0=lam_half[:], in1=halves[:], op=ALU.pow)
         c_flat = c_col[:].rearrange("p g t -> p (g t)")
         c_abs = keep.tile([P, 8], F32)
         nc.vector.scalar_tensor_tensor(out=c_abs[:], in0=c_flat, scalar=-1.0, in1=c_flat, op0=ALU.mult, op1=ALU.max)
-        c_neg = keep.tile([P, 8], BF16)
-        nc.vector.tensor_scalar(out=c_neg[:], in0=c_flat, scalar1=0.0, scalar2=None, op0=ALU.is_lt)
+        pre = keep.tile([P, 8], F32)
+        roots = keep.tile([P, 12], F32)
+        twice = keep.tile([P, 4], F32)
+        nc.vector.tensor_scalar(out=twice[:], in0=lam_col[:], scalar1=2.0, scalar2=None, op0=ALU.mult)
         nc.vector.tensor_scalar_max(out=c_abs[:], in0=c_abs[:], scalar1=1.2e-38)
-        c_sign = keep.tile([P, 2, 4], BF16)
-        nc.vector.scalar_tensor_tensor(
-            out=c_sign[:].rearrange("p g t -> p (g t)"), in0=c_flat, scalar=0.0, in1=c_neg[:], op0=ALU.is_gt, op1=ALU.subtract
-        )
+        nc.vector.reciprocal(out=pre[:, 0:4], in_=twice[:])
+        nc.vector.tensor_scalar(out=pre[:, 4:8], in0=lam_col[:], scalar1=0.5, scalar2=None, op0=ALU.mult)
+        nc.vector.tensor_copy(out=roots[:, 8:12], in_=pre[:, 0:4])
+        nc.gpsimd.tensor_tensor(out=roots[:, 0:8], in0=pre[:], in1=halves[:], op=ALU.pow)
         c_log = keep.tile([P, 8], F32)
         nc.scalar.activation(out=c_log[:], in_=c_abs[:], func=ACT.Ln)
-        warm = keep.tile([P, 1], F32)
-        nc.scalar.activation(out=warm[:], in_=c_log[:, 0:1], func=ACT.Exp)
+        nc.scalar.activation(out=warm[:, 1:2], in_=one[:], func=ACT.Exp)
+        c_neg = keep.tile([P, 8], BF16)
+        nc.vector.tensor_scalar(out=c_neg[:], in0=c_flat, scalar1=0.0, scalar2=None, op0=ALU.is_lt)
+        c_sign = keep.tile([P, 2, 4], BF16)
         c_off = keep.tile([P, 8], F32)
-        nc.vector.tensor_scalar(
-            out=c_off[:], in0=c_log[:], scalar1=DIST_SCALE / 2, scalar2=LOG_AMPLITUDE * DIST_SCALE / 2,
-            op0=ALU.mult, op1=ALU.add,
-        )
+
+        def c_finish():
+            nc.vector.scalar_tensor_tensor(
+                out=c_sign[:].rearrange("p g t -> p (g t)"), in0=c_flat, scalar=0.0, in1=c_neg[:], op0=ALU.is_gt, op1=ALU.subtract
+            )
+            nc.vector.tensor_scalar(
+                out=c_off[:], in0=c_log[:], scalar1=DIST_SCALE / 2, scalar2=LOG_AMPLITUDE * DIST_SCALE / 2,
+                op0=ALU.mult, op1=ALU.add,
+            )
 
         z_grp = keep.tile([P, N, 4], BF16, align_bytes=64)
         x_grp = keep.tile([P, Q, 4], BF16, align_bytes=64)
@@ -121,130 +125,104 @@ def tile_ardgaussianprocessmean_x2_kernel(
         z_scales = keep.tile([P, N], U8, align_bytes=64)
         x_codes = keep.tile([P, Q], U32, align_bytes=64)
         x_scales = keep.tile([P, Q], U8, align_bytes=64)
-        norm_ps = psum_n.tile([P, 16], F32)
         z_bias = keep.tile([P, 8], F32)
+        nz_half = keep.tile([P, 8], F32)
         nx_half = keep.tile([P, 8], F32)
         nx_row = keep.tile([P, Q], F32)
+        root_row = keep.tile([P, 3, D], F32)
+
+        zeros = keep.tile([P, 512], BF16)
+        nc.gpsimd.memset(zeros[:], 0.0)
+
+        def warm_pe(n):
+            for r in range(n):
+                ps = psum_2.tile([P, 512], F32, tag="ps2", name="ps")
+                nc.tensor.matmul(out=ps[:], lhsT=zeros[:, 0:P], rhs=zeros[:], start=True, stop=True)
 
         copy_on = {"V": nc.vector.tensor_copy, "S": nc.scalar.copy}
-
         turned = {}
+        scaled = {}
 
-        def turn_pair(name, raw):
-            tp = psum_t.tile([P, 2, 2, P], F32, tag="tp")
+        def root_spread(w):
+            sp = psum_t.tile([P, 4, P], F32, tag="tp", name="sp")
+            for t in range(4):
+                nc.tensor.transpose(sp[:, t, :], roots[:, 4 * w + t : 4 * w + t + 1].to_broadcast([P, P]), ident[:])
+            turned["root", w] = sp
+
+        def root_copy(w, on):
+            copy_on[on](
+                out=root_row[:, w, :].rearrange("m (p t) -> m p t", t=4), in_=turned["root", w][:].rearrange("m t p -> m p t")
+            )
+
+        def raw_pair(w, k):
+            return z_raw[:, k // 2, 2 * (k % 2) : 2 * (k % 2) + 2, :] if w == 0 else x_raw[:, 2 * k : 2 * k + 2, :]
+
+        def turn(w, k):
+            tp = psum_t.tile([P, 2, 2, P], F32, tag="tp", name="tp")
             for a in range(2):
-                words = raw[:, a, :].bitcast(F32)
+                words = raw_pair(w, k)[:, a, :].bitcast(F32)
                 for u in range(2):
                     nc.tensor.transpose(tp[:, a, u, :], words[:, u : 256 : 2], ident[:])
-            turned[name] = tp
+            turned[w, k] = tp
 
-        def pair_copy(name, grp, on):
-            tp = turned[name]
+        def turn_copy(w, k, on):
+            grp = (z_grp, x_grp)[w][:, 256 * k : 256 * k + 256, :]
             copy_on[on](
                 out=grp.bitcast(F32).rearrange("p (a r) u -> p a r u", a=2),
-                in_=tp[:].rearrange("p a u r -> p a r u"),
+                in_=turned[w, k][:].rearrange("p a u r -> p a r u"),
             )
 
-        def quant(grp, codes, scales):
+        def quant(w, c0, c1):
             nc.vector.quantize_mx(
-                out=codes.bitcast(FP8X4), scales=scales, in_=grp.rearrange("p r t -> p (r t)")
+                out=(z_codes, x_codes)[w][:, c0:c1].bitcast(FP8X4),
+                scales=(z_scales, x_scales)[w][:, c0:c1],
+                in_=(z_grp, x_grp)[w][:, c0:c1, :].rearrange("p r t -> p (r t)"),
             )
 
-        def z_turn(k):
-            turn_pair(("z", k), z_raw[:, k // 2, 2 * (k % 2) : 2 * (k % 2) + 2, :])
+        def scale(w, k, b, on):
+            y = work.tile([P, D], F32, tag="y" + on, bufs=4, name="y")
+            scaled[w, k, b] = y
+            eng = nc.gpsimd if on == "G" else nc.vector
+            eng.tensor_tensor(out=y[:], in0=raw_pair(w, k)[:, b, :], in1=root_row[:, w, :], op=ALU.mult)
 
-        def z_copy(k, on):
-            pair_copy(("z", k), z_grp[:, 256 * k : 256 * k + 256, :], on)
-
-        def x_turn(k):
-            turn_pair(("x", k), x_raw[:, 2 * k : 2 * k + 2, :])
-
-        def x_copy(k, on):
-            pair_copy(("x", k), x_grp[:, 256 * k : 256 * k + 256, :], on)
-
-        def z_quant(c0, c1):
-            quant(z_grp[:, c0:c1, :], z_codes[:, c0:c1], z_scales[:, c0:c1])
-
-        def x_quant(c0, c1):
-            quant(x_grp[:, c0:c1, :], x_codes[:, c0:c1], x_scales[:, c0:c1])
-
-        spreads = {}
-        root_row = keep.tile([P, D], F32)
-
-        def root_spread():
-            sp = psum_t.tile([P, 4, P], F32, tag="tp")
-            for t in range(4):
-                nc.tensor.matmul(
-                    out=sp[:, t, :], lhsT=root[:, t : t + 1].to_broadcast([P, P]), rhs=ident[:], start=True, stop=True
-                )
-            spreads["root"] = sp
-
-        def root_copy():
-            sp = spreads["root"]
-            nc.scalar.copy(out=root_row[:].rearrange("m (p t) -> m p t", t=4), in_=sp[:].rearrange("m t p -> m p t"))
-
-        def x_scaled(i):
-            y = work.tile([P, D], F32, tag="xl", bufs=3)
-            squares["row", i] = y
-            nc.gpsimd.tensor_tensor(out=y[:], in0=x_raw[:, i, :], in1=root_row[:], op=ALU.mult)
-
-        def x_norm(i):
+        def norm(w, k, b):
             junk = work.tile([P, D], F32, tag="junk", bufs=2)
-            nc.scalar.activation(out=junk[:], in_=squares["row", i][:], func=ACT.Square, accum_out=nx_half[:, i : i + 1])
+            j = 2 * k + b
+            nc.scalar.activation(
+                out=junk[:], in_=scaled[w, k, b][:], func=ACT.Square, accum_out=(nz_half, nx_half)[w][:, j : j + 1]
+            )
 
-        squares = {}
+        def square(k):
+            y = work.tile([P, 2, D], F32, tag="sq", bufs=2, name="y")
+            scaled["sq", k] = y
+            nc.scalar.activation(out=y[:], in_=raw_pair(0, k), func=ACT.Square)
 
-        def square(which, k, on):
-            grp = (z_grp if which == "z" else x_grp)[:, 256 * k : 256 * k + 256, :].rearrange("p r t -> p t r")
-            sq = work.tile([P, 4, 256], F32, tag="sq", bufs=4)
-            squares[which, k] = sq
-            if on == "S":
-                nc.scalar.activation(out=sq[:], in_=grp, func=ACT.Square)
-            else:
-                nc.gpsimd.tensor_tensor(out=sq[:], in0=grp, in1=grp, op=ALU.mult)
-
-        def norm_sum(which, k):
-            sq = squares[which, k]
-            for b in range(2):
-                col = 2 * k + b + (0 if which == "z" else 8)
-                for t in range(4):
-                    nc.tensor.matmul(
-                        out=norm_ps[:, col : col + 1],
-                        lhsT=sq[:, t, P * b : P * b + P],
-                        rhs=(lam_inv if which == "z" else lam_f)[:, t : t + 1],
-                        start=(t == 0),
-                        stop=(t == 3),
-                    )
-
-        def z_bias_of(g):
-            gc = slice(4 * g, 4 * g + 4)
+        def weigh(k, b):
+            junk = work.tile([P, D], F32, tag="vjunk", bufs=2)
+            j = 2 * k + b
             nc.vector.scalar_tensor_tensor(
-                out=z_bias[:, gc], in0=norm_ps[:, gc], scalar=-0.5, in1=c_off[:, gc], op0=ALU.mult, op1=ALU.add
+                out=junk[:], in0=scaled["sq", k][:, b, :], scalar=1.0, in1=root_row[:, 2, :], op0=ALU.mult, op1=ALU.mult,
+                accum_out=nz_half[:, j : j + 1],
             )
 
-        def x_half_of(k):
-            nc.vector.tensor_scalar(
-                out=nx_half[:, 2 * k : 2 * k + 2], in0=norm_ps[:, 8 + 2 * k : 10 + 2 * k], scalar1=0.5, scalar2=None, op0=ALU.mult
-            )
+        def bias(g):
+            gc = slice(4 * g, 4 * g + 4)
+            nc.vector.tensor_sub(out=z_bias[:, gc], in0=c_off[:, gc], in1=nz_half[:, gc])
 
-        def x_spread(k):
-            sp = psum_t.tile([P, 2, P], F32, tag="tp")
+        def spread(k):
+            sp = psum_t.tile([P, 2, P], F32, tag="tp", name="sp")
             for b in range(2):
                 i = 2 * k + b
-                nc.tensor.matmul(
-                    out=sp[:, b, :], lhsT=nx_half[:, i : i + 1].to_broadcast([P, P]), rhs=ident[:], start=True, stop=True
-                )
-            spreads[k] = sp
+                nc.tensor.transpose(sp[:, b, :], nx_half[:, i : i + 1].to_broadcast([P, P]), ident[:])
+            turned["spread", k] = sp
 
-        def x_spread_copy(k, on):
-            sp = spreads[k]
-            copy_on[on](out=nx_row[:, 256 * k : 256 * k + 256], in_=sp[:].rearrange("p k m -> p (k m)"))
+        def spread_copy(k, on):
+            copy_on[on](out=nx_row[:, 256 * k : 256 * k + 256], in_=turned["spread", k][:].rearrange("p k m -> p (k m)"))
 
         k_codes = keep.tile([P, 4, 2, 256], U32, align_bytes=64)
         k_scales = keep.tile([P, 4, 2, 256], U8, align_bytes=64)
         args = {}
         exps = {}
-
         scs = {}
 
         def score_mm(k, g, tt):
@@ -265,19 +243,18 @@ def tile_ardgaussianprocessmean_x2_kernel(
 
         def score_add(k, g, tt):
             cols = slice(256 * k, 256 * k + 256)
-            if tt == 0:
+            if (k, g) not in args:
                 args[k, g] = work.tile([P, 4, 256], F32, tag="arg", bufs=4, name="arg")
-            arg = args[k, g]
             ps = scs[k, g, tt]
             for b in range(2):
                 j = 4 * g + 2 * tt + b
                 nc.vector.scalar_tensor_tensor(
-                    out=arg[:, 2 * tt + b, :], in0=ps[:, b, :], scalar=z_bias[:, j : j + 1], in1=nx_row[:, cols],
+                    out=args[k, g][:, 2 * tt + b, :], in0=ps[:, b, :], scalar=z_bias[:, j : j + 1], in1=nx_row[:, cols],
                     op0=ALU.add, op1=ALU.subtract,
                 )
 
         def expo(k, g):
-            if g == 0:
+            if k not in exps:
                 exps[k] = work.tile([P, 2, 256, 4], BF16, tag="ex", bufs=3, align_bytes=64, name="ex")
             nc.scalar.activation(
                 out=exps[k][:, g, :, :], in_=args[k, g][:].rearrange("p t q -> p q t"), func=ACT.Exp, scale=2.0 / DIST_SCALE
@@ -295,6 +272,7 @@ def tile_ardgaussianprocessmean_x2_kernel(
             )
 
         rs = {}
+        stored = {}
         rbs = {}
         ps2s = {}
         tps = {}
@@ -302,7 +280,7 @@ def tile_ardgaussianprocessmean_x2_kernel(
 
         def product(i, g):
             cols = slice(P * i, P * i + P)
-            if g == 0:
+            if i not in rs:
                 rs[i] = work.tile([P, T], F32, tag="r", bufs=5, name="r")
                 rbs[i] = work.tile([P, 2, 2, P, 2], BF16, tag="rb", bufs=3, align_bytes=64, name="rb")
             ps = psum_2.tile([P, 512], F32, tag="ps2")
@@ -319,19 +297,23 @@ def tile_ardgaussianprocessmean_x2_kernel(
                     stop=(k == 2),
                 )
 
-        def r_out(i, g):
-            nc.scalar.copy(out=rs[i][:, 512 * g : 512 * g + 512], in_=ps2s[i, g][:])
-            if g == 1:
+        def r_out(i, g, on):
+            copy_on[on](out=rs[i][:, 512 * g : 512 * g + 512], in_=ps2s[i, g][:])
+            stored[i] = stored.get(i, 0) + 1
+            if stored[i] == 2:
                 nc.sync.dma_start(out=out_0[P * i : P * i + P, :], in_=rs[i][:])
 
-        def r_round(i, g):
-            nc.vector.tensor_copy(
-                out=rbs[i][:, g, :, :, :],
-                in_=rs[i][:, 512 * g : 512 * g + 512].rearrange("q (p u e) -> q u p e", u=2, e=2),
-            )
+        def r_round(i, g, on):
+            src = rs[i][:, 512 * g : 512 * g + 512].rearrange("q (p u e) -> q u p e", u=2, e=2)
+            if on == "V":
+                nc.vector.tensor_copy(out=rbs[i][:, g, :, :, :], in_=src)
+            else:
+                nc.gpsimd.tensor_scalar(
+                    out=rbs[i][:, g, :, :, :], in0=src, scalar1=1.0, scalar2=0.0, op0=ALU.mult, op1=ALU.add
+                )
 
         def r_turn(i, g):
-            if g == 0:
+            if i not in tps:
                 tps[i] = psum_t.tile([P, 2, 2, P], F32, tag="tp", name="tp")
             for u in range(2):
                 nc.tensor.transpose(
@@ -339,7 +321,7 @@ def tile_ardgaussianprocessmean_x2_kernel(
                 )
 
         def y_copy(i, on):
-            if i % 2 == 0:
+            if i // 2 not in ys:
                 ys[i // 2] = work.tile([P, 2, 256, 4], BF16, tag="y_grp", bufs=3, align_bytes=64, name="y_grp")
             a = i % 2
             copy_on[on](
@@ -364,114 +346,204 @@ def tile_ardgaussianprocessmean_x2_kernel(
                     out=out_2[:, 4 * b : 4 * b + 4, q0 : q0 + 256].rearrange("g q n -> q g n").bitcast(I32),
                     in_=y_scales[32 * b : 32 * b + 4, :, :].bitcast(I32),
                 )
-
-        z_turn(0)
-        z_turn(1)
-        root_spread()
-        root_copy()
-        z_copy(0, "V")
-        square("z", 0, "S")
-        z_copy(1, "V")
-        square("z", 1, "S")
-        x_turn(0)
-        x_copy(0, "V")
-        z_quant(0, 512)
-        x_scaled(0)
-        x_scaled(1)
-        norm_sum("z", 0)
-        norm_sum("z", 1)
-        z_bias_of(0)
-        x_quant(0, 256)
-        x_norm(0)
-        x_norm(1)
-        z_turn(2)
-        z_copy(2, "V")
-        square("z", 2, "S")
-        x_spread(0)
-        x_spread_copy(0, "S")
-        score_mm(0, 0, 0)
+        square(1)
+        root_spread(1)
+        root_spread(2)
+        root_copy(1, "S")
+        root_copy(2, "S")
+        warm_pe(2)
+        root_spread(0)
+        turn(0, 0)
+        scale(1, 0, 1, "G")
+        root_copy(0, "S")
+        warm_pe(6)
+        square(0)
+        weigh(1, 0)
+        turn(0, 1)
+        weigh(1, 1)
+        turn_copy(0, 0, "V")
+        turn(1, 0)
+        scale(1, 0, 0, "G")
+        weigh(0, 0)
+        turn_copy(0, 1, "V")
+        turn_copy(1, 0, "V")
+        scale(0, 3, 0, "G")
+        norm(1, 0, 1)
+        turn(0, 2)
+        norm(0, 3, 0)
+        norm(1, 0, 0)
+        quant(1, 0, 256)
+        warm_pe(1)
+        spread(0)
+        warm_pe(1)
+        scale(0, 2, 0, "G")
+        turn_copy(0, 2, "S")
+        scale(0, 2, 1, "G")
+        turn(0, 3)
+        spread_copy(0, "S")
+        norm(0, 2, 1)
+        scale(0, 3, 1, "G")
+        quant(0, 0, 512)
+        norm(0, 2, 0)
+        scale(1, 1, 1, "G")
+        norm(0, 3, 1)
+        turn(1, 1)
+        scale(1, 1, 0, "G")
+        scale(1, 2, 0, "G")
+        c_finish()
+        norm(1, 1, 1)
+        scale(1, 3, 0, "G")
         score_mm(0, 0, 1)
-        z_turn(3)
-        z_copy(3, "V")
-        square("z", 3, "S")
-        score_add(0, 0, 0)
+        weigh(0, 1)
+        scale(1, 3, 1, "G")
+        turn_copy(0, 3, "V")
+        turn(1, 3)
+        bias(0)
+        turn_copy(1, 1, "S")
+        score_mm(0, 0, 0)
+        quant(0, 512, 1024)
         score_add(0, 0, 1)
-        x_scaled(2)
-        x_scaled(3)
-        norm_sum("z", 2)
-        x_turn(1)
-        z_quant(512, 1024)
-        expo(0, 0)
-        norm_sum("z", 3)
-        z_bias_of(1)
-        x_copy(1, "S")
-        x_norm(2)
-        x_norm(3)
-        x_quant(256, 512)
-        score_mm(0, 1, 0)
         score_mm(0, 1, 1)
-        x_spread(1)
-        x_spread_copy(1, "S")
-        score_add(0, 1, 0)
+        bias(1)
+        warm_pe(1)
+        norm(1, 1, 0)
+        score_mm(0, 1, 0)
+        score_add(0, 0, 0)
+        spread(1)
+        turn_copy(1, 3, "S")
+        expo(0, 0)
+        scale(1, 2, 1, "G")
         score_add(0, 1, 1)
-        x_turn(2)
-        x_copy(2, "S")
-        square("x", 2, "G")
+        quant(1, 256, 512)
+        score_mm(1, 1, 0)
+        score_add(0, 1, 0)
+        spread_copy(1, "S")
         score_mm(1, 0, 0)
-        score_mm(1, 0, 1)
+        score_add(1, 1, 0)
         expo(0, 1)
-        x_turn(3)
-        x_copy(3, "S")
-        square("x", 3, "G")
+        turn(1, 2)
+        turn_copy(1, 2, "S")
+        norm(1, 2, 0)
         sign(0, 0)
         score_add(1, 0, 0)
-        score_add(1, 0, 1)
-        x_quant(512, 1024)
-        score_mm(1, 1, 0)
-        score_mm(1, 1, 1)
-        expo(1, 0)
+        score_mm(1, 0, 1)
+        norm(1, 2, 1)
+        norm(1, 3, 1)
         sign(0, 1)
+        score_add(1, 0, 1)
+        score_mm(1, 1, 1)
         k_quant(0)
-        norm_sum("x", 2)
-        x_half_of(2)
-        x_spread(2)
-        x_spread_copy(2, "S")
-        score_add(1, 1, 0)
+        spread(2)
+        quant(1, 512, 1024)
+        expo(1, 0)
+        spread_copy(2, "S")
+        product(0, 0)
+        score_mm(2, 0, 0)
+        r_out(0, 0, "S")
+        sign(1, 0)
+        norm(1, 3, 0)
         score_add(1, 1, 1)
-        for j in range(3, 13):
-            i = j - 3
-            if i < 8:
-                product(i, 0)
-            h = j + 1
-            if h < 8:
-                score_mm(h // 2, h % 2, 0)
-                score_mm(h // 2, h % 2, 1)
-            if 3 <= h + 0 and h - 1 < 8:
-                expo((h - 1) // 2, (h - 1) % 2)
-            if i < 8:
-                r_out(i, 0)
-                product(i, 1)
-            if h < 8:
-                score_add(h // 2, h % 2, 0)
-            if h - 2 < 8:
-                sign((h - 2) // 2, (h - 2) % 2)
-                if (h - 2) % 2 == 1:
-                    k_quant((h - 2) // 2)
-            if i < 8:
-                r_round(i, 0)
-            if h < 8:
-                score_add(h // 2, h % 2, 1)
-            if i < 8:
-                r_out(i, 1)
-                r_round(i, 1)
-            if j == 3:
-                norm_sum("x", 3)
-                x_half_of(3)
-                x_spread(3)
-                x_spread_copy(3, "S")
-            if 1 <= i < 9:
-                r_turn(i - 1, 0)
-                r_turn(i - 1, 1)
-                y_copy(i - 1, "SSSSVVVV"[i - 1])
-            if i >= 2 and i % 2 == 0:
-                y_quant(i // 2 - 1)
+        score_add(2, 0, 0)
+        score_mm(2, 1, 1)
+        product(0, 1)
+        expo(1, 1)
+        product(1, 0)
+        score_mm(2, 0, 1)
+        score_mm(2, 1, 0)
+        r_out(0, 1, "S")
+        r_out(1, 0, "S")
+        spread(3)
+        score_add(2, 1, 1)
+        score_add(2, 0, 1)
+        sign(1, 1)
+        score_mm(3, 0, 1)
+        expo(2, 0)
+        spread_copy(3, "S")
+        product(1, 1)
+        k_quant(1)
+        score_mm(3, 0, 0)
+        r_round(0, 0, "G")
+        r_round(0, 1, "G")
+        score_add(2, 1, 0)
+        sign(2, 0)
+        product(3, 0)
+        product(2, 0)
+        score_mm(3, 1, 0)
+        r_turn(0, 0)
+        r_out(1, 1, "S")
+        score_add(3, 0, 1)
+        score_add(3, 0, 0)
+        r_round(1, 1, "G")
+        score_add(3, 1, 0)
+        expo(2, 1)
+        score_mm(3, 1, 1)
+        sign(2, 1)
+        product(2, 1)
+        r_out(3, 0, "S")
+        r_out(2, 0, "S")
+        r_round(1, 0, "G")
+        r_out(2, 1, "S")
+        r_turn(1, 1)
+        r_round(3, 0, "G")
+        r_turn(0, 1)
+        score_add(3, 1, 1)
+        k_quant(2)
+        product(3, 1)
+        r_round(2, 1, "G")
+        r_turn(1, 0)
+        y_copy(0, "V")
+        expo(3, 1)
+        r_out(3, 1, "S")
+        sign(3, 1)
+        y_copy(1, "V")
+        product(4, 0)
+        r_round(2, 0, "G")
+        expo(3, 0)
+        product(4, 1)
+        y_quant(0)
+        r_out(4, 0, "S")
+        sign(3, 0)
+        r_out(4, 1, "S")
+        r_round(3, 1, "G")
+        product(5, 0)
+        k_quant(3)
+        r_round(4, 1, "G")
+        r_turn(3, 1)
+        r_turn(2, 0)
+        r_turn(2, 1)
+        r_turn(3, 0)
+        product(5, 1)
+        y_copy(3, "V")
+        r_round(4, 0, "G")
+        product(6, 1)
+        r_out(5, 0, "S")
+        product(6, 0)
+        r_turn(4, 0)
+        y_copy(2, "V")
+        r_out(5, 1, "S")
+        y_quant(1)
+        r_round(5, 1, "G")
+        r_round(5, 0, "G")
+        r_turn(5, 1)
+        r_turn(4, 1)
+        r_out(6, 0, "S")
+        r_turn(5, 0)
+        y_copy(5, "V")
+        r_out(6, 1, "S")
+        product(7, 0)
+        r_out(7, 0, "S")
+        product(7, 1)
+        y_copy(4, "V")
+        y_quant(2)
+        r_round(6, 0, "G")
+        r_round(7, 0, "V")
+        r_round(6, 1, "G")
+        r_out(7, 1, "S")
+        r_turn(6, 1)
+        r_round(7, 1, "V")
+        r_turn(6, 0)
+        r_turn(7, 0)
+        r_turn(7, 1)
+        y_copy(6, "V")
+        y_copy(7, "V")
+        y_quant(3)

@@ -28,15 +28,15 @@ def tile_ardgaussianprocessmean_x2_kernel(
     with ExitStack() as ctx:
         keep = ctx.enter_context(tc.tile_pool(name="keep", bufs=1))
         work = ctx.enter_context(tc.tile_pool(name="work", bufs=2))
-        psum_t = ctx.enter_context(tc.psum_pool(name="psum_t", bufs=2))
-        psum_1 = ctx.enter_context(tc.psum_pool(name="psum_1", bufs=3))
+        psum_t = ctx.enter_context(tc.psum_pool(name="psum_t", bufs=3))
+        psum_1 = ctx.enter_context(tc.psum_pool(name="psum_1", bufs=2))
         psum_2 = ctx.enter_context(tc.psum_pool(name="psum_2", bufs=3))
         ctx.enter_context(tc.manual_schedule())
 
         lam_col = keep.tile([P, 4], BF16)
+        nc.scalar.dma_start(out=lam_col[:], in_=lam.rearrange("(p t) -> p t", t=4))
         c_col = keep.tile([P, 2, 4], BF16)
         nc.scalar.dma_start(out=c_col[:], in_=c.rearrange("(g m t) -> m g t", g=2, t=4))
-        nc.scalar.dma_start(out=lam_col[:], in_=lam.rearrange("(p t) -> p t", t=4))
 
         z_raw = keep.tile([P, 2, 4, D], BF16, align_bytes=64)
         x_raw = keep.tile([P, 8, D], BF16, align_bytes=64)
@@ -68,10 +68,10 @@ def tile_ardgaussianprocessmean_x2_kernel(
         for g in range(2):
             nc.sync.dma_start(out=w_words[:, 1 + g, :].bitcast(I32), in_=alpha_words[g].bitcast(I32))
 
+        zeros = keep.tile([P, 512], BF16)
+        nc.vector.memset(zeros[:], 0.0)
         one = keep.tile([P, 1], F32)
         nc.vector.memset(one[:], 1.0)
-        halves = keep.tile([P, 8], F32)
-        nc.vector.memset(halves[:], 0.5)
         warm = keep.tile([P, 2], F32)
         nc.scalar.activation(out=warm[:, 0:1], in_=one[:], func=ACT.Ln)
         ident = keep.tile([P, P], F32)
@@ -90,25 +90,61 @@ def tile_ardgaussianprocessmean_x2_kernel(
                 in_=alpha_scales[:, rows, :].rearrange("g q n -> q g n").bitcast(I32),
             )
 
+        lam_f = keep.tile([P, 4], F32)
+        nc.vector.tensor_copy(out=lam_f[:], in_=lam_col[:])
+        lam_two = keep.tile([P, 4], F32)
+        nc.vector.tensor_scalar(out=lam_two[:], in0=lam_col[:], scalar1=2.0, scalar2=None, op0=ALU.mult)
+        inv_half = keep.tile([P, 4], F32)
+        nc.vector.reciprocal(out=inv_half[:], in_=lam_two[:])
+        diag = keep.tile([P, 4, P], BF16)
+        halves = keep.tile([P, 4], F32)
+        nc.vector.memset(halves[:], 0.5)
+        lam_half = keep.tile([P, 4], F32)
+        nc.vector.tensor_scalar(out=lam_half[:], in0=lam_col[:], scalar1=0.5, scalar2=None, op0=ALU.mult)
+        roots = keep.tile([P, 2, 4], F32)
+        diag_2 = keep.tile([P, 2, 2, 4, P], BF16)
+
+        def root_of(w):
+            nc.gpsimd.tensor_tensor(out=roots[:, w, :], in0=(inv_half, lam_half)[w][:], in1=halves[:], op=ALU.pow)
+
+        root_of(0)
+
+
+        def diag_hi(w, t):
+            nc.vector.tensor_scalar(
+                out=diag_2[:, w, 0, t, :], in0=ident[:], scalar1=roots[:, w, t : t + 1], scalar2=None, op0=ALU.mult
+            )
+
+        def diag_lo(w, t):
+            nc.vector.scalar_tensor_tensor(
+                out=diag_2[:, w, 1, t, :], in0=ident[:], scalar=roots[:, w, t : t + 1], in1=diag_2[:, w, 0, t, :],
+                op0=ALU.mult, op1=ALU.subtract,
+            )
+
+
+        def warm_pe(n):
+            for r in range(n):
+                ps = psum_2.tile([P, 512], F32, tag="ps2", name="ps")
+                nc.tensor.matmul(out=ps[:], lhsT=zeros[:, 0:P], rhs=zeros[:], start=True, stop=True)
+
+        def diag_of(t):
+            nc.vector.tensor_scalar(out=diag[:, t, :], in0=ident[:], scalar1=lam_f[:, t : t + 1], scalar2=None, op0=ALU.mult)
+
         c_flat = c_col[:].rearrange("p g t -> p (g t)")
         c_abs = keep.tile([P, 8], F32)
-        nc.vector.scalar_tensor_tensor(out=c_abs[:], in0=c_flat, scalar=-1.0, in1=c_flat, op0=ALU.mult, op1=ALU.max)
-        pre = keep.tile([P, 8], F32)
-        roots = keep.tile([P, 12], F32)
-        twice = keep.tile([P, 4], F32)
-        nc.vector.tensor_scalar(out=twice[:], in0=lam_col[:], scalar1=2.0, scalar2=None, op0=ALU.mult)
-        nc.vector.tensor_scalar_max(out=c_abs[:], in0=c_abs[:], scalar1=1.2e-38)
-        nc.vector.reciprocal(out=pre[:, 0:4], in_=twice[:])
-        nc.vector.tensor_scalar(out=pre[:, 4:8], in0=lam_col[:], scalar1=0.5, scalar2=None, op0=ALU.mult)
-        nc.vector.tensor_copy(out=roots[:, 8:12], in_=pre[:, 0:4])
-        nc.gpsimd.tensor_tensor(out=roots[:, 0:8], in0=pre[:], in1=halves[:], op=ALU.pow)
-        c_log = keep.tile([P, 8], F32)
-        nc.scalar.activation(out=c_log[:], in_=c_abs[:], func=ACT.Ln)
-        nc.scalar.activation(out=warm[:, 1:2], in_=one[:], func=ACT.Exp)
         c_neg = keep.tile([P, 8], BF16)
-        nc.vector.tensor_scalar(out=c_neg[:], in0=c_flat, scalar1=0.0, scalar2=None, op0=ALU.is_lt)
+        c_log = keep.tile([P, 8], F32)
         c_sign = keep.tile([P, 2, 4], BF16)
         c_off = keep.tile([P, 8], F32)
+
+        def c_start():
+            nc.vector.scalar_tensor_tensor(out=c_abs[:], in0=c_flat, scalar=-1.0, in1=c_flat, op0=ALU.mult, op1=ALU.max)
+            nc.vector.tensor_scalar(out=c_neg[:], in0=c_flat, scalar1=0.0, scalar2=None, op0=ALU.is_lt)
+            nc.vector.tensor_scalar_max(out=c_abs[:], in0=c_abs[:], scalar1=1.2e-38)
+
+        def ln_c():
+            nc.scalar.activation(out=c_log[:], in_=c_abs[:], func=ACT.Ln)
+            nc.scalar.activation(out=warm[:, 1:2], in_=one[:], func=ACT.Exp)
 
         def c_finish():
             nc.vector.scalar_tensor_tensor(
@@ -129,29 +165,22 @@ def tile_ardgaussianprocessmean_x2_kernel(
         nz_half = keep.tile([P, 8], F32)
         nx_half = keep.tile([P, 8], F32)
         nx_row = keep.tile([P, Q], F32)
-        root_row = keep.tile([P, 3, D], F32)
-
-        zeros = keep.tile([P, 512], BF16)
-        nc.gpsimd.memset(zeros[:], 0.0)
-
-        def warm_pe(n):
-            for r in range(n):
-                ps = psum_2.tile([P, 512], F32, tag="ps2", name="ps")
-                nc.tensor.matmul(out=ps[:], lhsT=zeros[:, 0:P], rhs=zeros[:], start=True, stop=True)
 
         copy_on = {"V": nc.vector.tensor_copy, "S": nc.scalar.copy}
         turned = {}
         scaled = {}
 
-        def root_spread(w):
+        inv_row = keep.tile([P, D], F32)
+
+        def inv_spread():
             sp = psum_t.tile([P, 4, P], F32, tag="tp", name="sp")
             for t in range(4):
-                nc.tensor.transpose(sp[:, t, :], roots[:, 4 * w + t : 4 * w + t + 1].to_broadcast([P, P]), ident[:])
-            turned["root", w] = sp
+                nc.tensor.transpose(sp[:, t, :], inv_half[:, t : t + 1].to_broadcast([P, P]), ident[:])
+            turned["inv"] = sp
 
-        def root_copy(w, on):
+        def inv_copy(on):
             copy_on[on](
-                out=root_row[:, w, :].rearrange("m (p t) -> m p t", t=4), in_=turned["root", w][:].rearrange("m t p -> m p t")
+                out=inv_row[:].rearrange("m (p t) -> m p t", t=4), in_=turned["inv"][:].rearrange("m t p -> m p t")
             )
 
         def raw_pair(w, k):
@@ -179,17 +208,37 @@ def tile_ardgaussianprocessmean_x2_kernel(
                 in_=(z_grp, x_grp)[w][:, c0:c1, :].rearrange("p r t -> p (r t)"),
             )
 
-        def scale(w, k, b, on):
-            y = work.tile([P, D], F32, tag="y" + on, bufs=4, name="y")
-            scaled[w, k, b] = y
-            eng = nc.gpsimd if on == "G" else nc.vector
-            eng.tensor_tensor(out=y[:], in0=raw_pair(w, k)[:, b, :], in1=root_row[:, w, :], op=ALU.mult)
+        def wx(i):
+            ps = psum_t.tile([P, 4, P], F32, tag="tp", name="sp")
+            for t in range(4):
+                nc.tensor.matmul(
+                    out=ps[:, t, :], lhsT=x_grp[:, P * i : P * i + P, t], rhs=diag[:, t, :], start=True, stop=True
+                )
+            turned["wx", i] = ps
 
-        def norm(w, k, b):
-            junk = work.tile([P, D], F32, tag="junk", bufs=2)
-            j = 2 * k + b
+        def times_root(w, j):
+            ps = psum_t.tile([P, 4, P], F32, tag="tp", name="sp")
+            for t in range(4):
+                for term in range(2):
+                    nc.tensor.matmul(
+                        out=ps[:, t, :], lhsT=(z_grp, x_grp)[w][:, P * j : P * j + P, t], rhs=diag_2[:, w, term, t, :],
+                        start=(term == 0), stop=(term == 1),
+                    )
+            turned["root", w, j] = ps
+
+        def root_sum(w, j):
+            junk = work.tile([P, D], F32, tag="sjunk", bufs=2)
             nc.scalar.activation(
-                out=junk[:], in_=scaled[w, k, b][:], func=ACT.Square, accum_out=(nz_half, nx_half)[w][:, j : j + 1]
+                out=junk[:], in_=turned["root", w, j][:].rearrange("q t p -> q (t p)"), func=ACT.Square,
+                accum_out=(nz_half, nx_half)[w][:, j : j + 1],
+            )
+
+        def xsum(i):
+            junk = work.tile([P, D], F32, tag="vjunk", bufs=2)
+            nc.vector.scalar_tensor_tensor(
+                out=junk[:].rearrange("q (p t) -> q p t", t=4), in0=turned["wx", i][:].rearrange("q t p -> q p t"), scalar=0.5,
+                in1=x_raw[:, i, :].rearrange("q (p t) -> q p t", t=4),
+                op0=ALU.mult, op1=ALU.mult, accum_out=nx_half[:, i : i + 1],
             )
 
         def square(k):
@@ -201,7 +250,7 @@ def tile_ardgaussianprocessmean_x2_kernel(
             junk = work.tile([P, D], F32, tag="vjunk", bufs=2)
             j = 2 * k + b
             nc.vector.scalar_tensor_tensor(
-                out=junk[:], in0=scaled["sq", k][:, b, :], scalar=1.0, in1=root_row[:, 2, :], op0=ALU.mult, op1=ALU.mult,
+                out=junk[:], in0=scaled["sq", k][:, b, :], scalar=1.0, in1=inv_row[:], op0=ALU.mult, op1=ALU.mult,
                 accum_out=nz_half[:, j : j + 1],
             )
 
@@ -257,7 +306,8 @@ def tile_ardgaussianprocessmean_x2_kernel(
             if k not in exps:
                 exps[k] = work.tile([P, 2, 256, 4], BF16, tag="ex", bufs=3, align_bytes=64, name="ex")
             nc.scalar.activation(
-                out=exps[k][:, g, :, :], in_=args[k, g][:].rearrange("p t q -> p q t"), func=ACT.Exp, scale=2.0 / DIST_SCALE
+                out=exps[k][:, g, :, :].rearrange("p (c i) t -> p c t i", i=4),
+                in_=args[k, g][:].rearrange("p t (c i) -> p c t i", i=4), func=ACT.Exp, scale=2.0 / DIST_SCALE
             )
 
         def sign(k, g):
@@ -312,13 +362,13 @@ def tile_ardgaussianprocessmean_x2_kernel(
                     out=rbs[i][:, g, :, :, :], in0=src, scalar1=1.0, scalar2=0.0, op0=ALU.mult, op1=ALU.add
                 )
 
-        def r_turn(i, g):
-            if i not in tps:
-                tps[i] = psum_t.tile([P, 2, 2, P], F32, tag="tp", name="tp")
-            for u in range(2):
-                nc.tensor.transpose(
-                    tps[i][:, g, u, :], rbs[i][:, g, u, :, :].rearrange("q p e -> q (p e)").bitcast(F32), ident[:]
-                )
+        def r_turn(i):
+            tps[i] = psum_t.tile([P, 2, 2, P], F32, tag="tp", name="tp")
+            for g in range(2):
+                for u in range(2):
+                    nc.tensor.transpose(
+                        tps[i][:, g, u, :], rbs[i][:, g, u, :, :].rearrange("q p e -> q (p e)").bitcast(F32), ident[:]
+                    )
 
         def y_copy(i, on):
             if i // 2 not in ys:
@@ -346,204 +396,202 @@ def tile_ardgaussianprocessmean_x2_kernel(
                     out=out_2[:, 4 * b : 4 * b + 4, q0 : q0 + 256].rearrange("g q n -> q g n").bitcast(I32),
                     in_=y_scales[32 * b : 32 * b + 4, :, :].bitcast(I32),
                 )
-        square(1)
-        root_spread(1)
-        root_spread(2)
-        root_copy(1, "S")
-        root_copy(2, "S")
-        warm_pe(2)
-        root_spread(0)
-        turn(0, 0)
-        scale(1, 0, 1, "G")
-        root_copy(0, "S")
-        warm_pe(6)
         square(0)
-        weigh(1, 0)
+        turn(0, 0)
         turn(0, 1)
-        weigh(1, 1)
+        square(1)
         turn_copy(0, 0, "V")
+        root_of(0)
+        diag_of(2)
+        diag_of(3)
+        diag_hi(0, 0)
+        diag_hi(0, 1)
         turn(1, 0)
-        scale(1, 0, 0, "G")
-        weigh(0, 0)
-        turn_copy(0, 1, "V")
-        turn_copy(1, 0, "V")
-        scale(0, 3, 0, "G")
-        norm(1, 0, 1)
-        turn(0, 2)
-        norm(0, 3, 0)
-        norm(1, 0, 0)
-        quant(1, 0, 256)
-        warm_pe(1)
-        spread(0)
-        warm_pe(1)
-        scale(0, 2, 0, "G")
-        turn_copy(0, 2, "S")
-        scale(0, 2, 1, "G")
-        turn(0, 3)
-        spread_copy(0, "S")
-        norm(0, 2, 1)
-        scale(0, 3, 1, "G")
+        c_start()
+        turn_copy(0, 1, "S")
+        diag_lo(0, 0)
+        diag_lo(0, 1)
+        diag_of(1)
+        diag_hi(0, 3)
+        diag_of(0)
+        ln_c()
+        diag_hi(0, 2)
         quant(0, 0, 512)
-        norm(0, 2, 0)
-        scale(1, 1, 1, "G")
-        norm(0, 3, 1)
-        turn(1, 1)
-        scale(1, 1, 0, "G")
-        scale(1, 2, 0, "G")
+        inv_spread()
+        diag_lo(0, 2)
+        diag_lo(0, 3)
+        turn_copy(1, 0, "V")
+        turn(0, 2)
+        inv_copy("S")
         c_finish()
-        norm(1, 1, 1)
-        scale(1, 3, 0, "G")
+        quant(1, 0, 256)
+        weigh(1, 0)
+        wx(0)
+        turn_copy(0, 2, "S")
+        weigh(1, 1)
+        wx(1)
+        xsum(0)
+        score_mm(0, 0, 0)
+        xsum(1)
         score_mm(0, 0, 1)
         weigh(0, 1)
-        scale(1, 3, 1, "G")
-        turn_copy(0, 3, "V")
-        turn(1, 3)
+        spread(0)
+        turn(0, 3)
+        weigh(0, 0)
+        spread_copy(0, "S")
+        turn(1, 1)
+        turn_copy(0, 3, "S")
         bias(0)
-        turn_copy(1, 1, "S")
-        score_mm(0, 0, 0)
-        quant(0, 512, 1024)
-        score_add(0, 0, 1)
-        score_mm(0, 1, 1)
-        bias(1)
-        warm_pe(1)
-        norm(1, 1, 0)
-        score_mm(0, 1, 0)
+        times_root(0, 5)
         score_add(0, 0, 0)
-        spread(1)
-        turn_copy(1, 3, "S")
-        expo(0, 0)
-        scale(1, 2, 1, "G")
-        score_add(0, 1, 1)
+        turn_copy(1, 1, "S")
+        times_root(0, 4)
+        quant(0, 512, 1024)
+        root_sum(0, 5)
+        wx(2)
+        score_add(0, 0, 1)
+        root_sum(0, 4)
+        score_mm(0, 1, 0)
+        wx(3)
         quant(1, 256, 512)
-        score_mm(1, 1, 0)
-        score_add(0, 1, 0)
-        spread_copy(1, "S")
-        score_mm(1, 0, 0)
-        score_add(1, 1, 0)
-        expo(0, 1)
-        turn(1, 2)
-        turn_copy(1, 2, "S")
-        norm(1, 2, 0)
+        expo(0, 0)
+        times_root(0, 6)
+        xsum(2)
+        score_mm(0, 1, 1)
+        xsum(3)
+        times_root(0, 7)
+        root_sum(0, 6)
         sign(0, 0)
-        score_add(1, 0, 0)
+        spread(1)
+        root_sum(0, 7)
+        turn(1, 2)
+        spread_copy(1, "S")
+        bias(1)
+        turn(1, 3)
+        turn_copy(1, 2, "S")
+        score_add(0, 1, 1)
+        turn_copy(1, 3, "S")
+        score_add(0, 1, 0)
+        wx(5)
+        wx(4)
+        xsum(5)
+        wx(6)
+        expo(0, 1)
+        score_mm(1, 0, 0)
+        xsum(4)
         score_mm(1, 0, 1)
-        norm(1, 2, 1)
-        norm(1, 3, 1)
-        sign(0, 1)
-        score_add(1, 0, 1)
-        score_mm(1, 1, 1)
-        k_quant(0)
+        wx(7)
+        score_add(1, 0, 0)
         spread(2)
-        quant(1, 512, 1024)
-        expo(1, 0)
+        score_add(1, 0, 1)
         spread_copy(2, "S")
+        score_mm(1, 1, 1)
+        sign(0, 1)
+        expo(1, 0)
+        score_mm(1, 1, 0)
+        quant(1, 512, 1024)
+        k_quant(0)
+        score_add(1, 1, 0)
         product(0, 0)
-        score_mm(2, 0, 0)
+        score_add(1, 1, 1)
+        product(0, 1)
         r_out(0, 0, "S")
         sign(1, 0)
-        norm(1, 3, 0)
-        score_add(1, 1, 1)
-        score_add(2, 0, 0)
-        score_mm(2, 1, 1)
-        product(0, 1)
         expo(1, 1)
-        product(1, 0)
+        xsum(6)
+        score_mm(2, 0, 0)
         score_mm(2, 0, 1)
-        score_mm(2, 1, 0)
+        score_add(2, 0, 0)
+        product(1, 0)
         r_out(0, 1, "S")
-        r_out(1, 0, "S")
-        spread(3)
-        score_add(2, 1, 1)
-        score_add(2, 0, 1)
         sign(1, 1)
-        score_mm(3, 0, 1)
-        expo(2, 0)
-        spread_copy(3, "S")
+        score_mm(2, 1, 0)
+        r_out(1, 0, "S")
         product(1, 1)
+        score_add(2, 0, 1)
         k_quant(1)
-        score_mm(3, 0, 0)
-        r_round(0, 0, "G")
-        r_round(0, 1, "G")
+        expo(2, 0)
+        score_mm(2, 1, 1)
         score_add(2, 1, 0)
-        sign(2, 0)
-        product(3, 0)
         product(2, 0)
-        score_mm(3, 1, 0)
-        r_turn(0, 0)
+        r_round(0, 0, "V")
         r_out(1, 1, "S")
-        score_add(3, 0, 1)
-        score_add(3, 0, 0)
-        r_round(1, 1, "G")
-        score_add(3, 1, 0)
-        expo(2, 1)
-        score_mm(3, 1, 1)
-        sign(2, 1)
-        product(2, 1)
-        r_out(3, 0, "S")
+        score_add(2, 1, 1)
+        score_mm(3, 0, 1)
         r_out(2, 0, "S")
-        r_round(1, 0, "G")
+        product(2, 1)
+        xsum(7)
+        expo(2, 1)
+        r_round(0, 1, "V")
+        score_mm(3, 0, 0)
+        sign(2, 0)
+        spread(3)
+        r_turn(0)
         r_out(2, 1, "S")
-        r_turn(1, 1)
-        r_round(3, 0, "G")
-        r_turn(0, 1)
-        score_add(3, 1, 1)
-        k_quant(2)
+        r_round(1, 0, "V")
+        product(3, 0)
+        r_round(1, 1, "V")
+        spread_copy(3, "S")
+        sign(2, 1)
+        y_copy(0, "S")
+        r_turn(1)
+        score_add(3, 0, 0)
+        r_out(3, 0, "S")
         product(3, 1)
-        r_round(2, 1, "G")
-        r_turn(1, 0)
-        y_copy(0, "V")
-        expo(3, 1)
-        r_out(3, 1, "S")
-        sign(3, 1)
-        y_copy(1, "V")
-        product(4, 0)
-        r_round(2, 0, "G")
+        score_add(3, 0, 1)
+        y_copy(1, "S")
+        k_quant(2)
+        score_mm(3, 1, 1)
         expo(3, 0)
-        product(4, 1)
+        score_mm(3, 1, 0)
         y_quant(0)
+        product(4, 0)
+        score_add(3, 1, 0)
+        r_out(3, 1, "S")
+        product(4, 1)
+        r_round(2, 0, "V")
         r_out(4, 0, "S")
-        sign(3, 0)
-        r_out(4, 1, "S")
-        r_round(3, 1, "G")
+        score_add(3, 1, 1)
         product(5, 0)
-        k_quant(3)
-        r_round(4, 1, "G")
-        r_turn(3, 1)
-        r_turn(2, 0)
-        r_turn(2, 1)
-        r_turn(3, 0)
+        r_out(4, 1, "S")
+        r_round(2, 1, "V")
+        sign(3, 0)
+        expo(3, 1)
+        r_turn(2)
+        r_round(3, 0, "V")
         product(5, 1)
-        y_copy(3, "V")
-        r_round(4, 0, "G")
-        product(6, 1)
+        r_round(3, 1, "V")
+        r_round(4, 0, "V")
+        y_copy(2, "S")
+        sign(3, 1)
+        r_turn(3)
         r_out(5, 0, "S")
+        r_round(4, 1, "V")
+        k_quant(3)
+        r_turn(4)
+        y_copy(3, "S")
+        r_round(5, 0, "V")
         product(6, 0)
-        r_turn(4, 0)
-        y_copy(2, "V")
-        r_out(5, 1, "S")
+        y_copy(4, "S")
         y_quant(1)
-        r_round(5, 1, "G")
-        r_round(5, 0, "G")
-        r_turn(5, 1)
-        r_turn(4, 1)
+        r_out(5, 1, "S")
+        product(6, 1)
         r_out(6, 0, "S")
-        r_turn(5, 0)
-        y_copy(5, "V")
+        r_round(5, 1, "V")
+        r_turn(5)
+        r_round(6, 0, "V")
         r_out(6, 1, "S")
         product(7, 0)
-        r_out(7, 0, "S")
+        y_copy(5, "S")
+        r_round(6, 1, "V")
         product(7, 1)
-        y_copy(4, "V")
         y_quant(2)
-        r_round(6, 0, "G")
+        r_out(7, 0, "S")
+        r_turn(6)
         r_round(7, 0, "V")
-        r_round(6, 1, "G")
         r_out(7, 1, "S")
-        r_turn(6, 1)
+        y_copy(6, "S")
         r_round(7, 1, "V")
-        r_turn(6, 0)
-        r_turn(7, 0)
-        r_turn(7, 1)
-        y_copy(6, "V")
-        y_copy(7, "V")
+        r_turn(7)
+        y_copy(7, "S")
         y_quant(3)

from contextlib import ExitStack

import concourse.mybir as mybir
from concourse.masks import make_identity

Q, N, D, T = 1024, 1024, 512, 1024
FLOPS = 2 * (Q * N * D + Q * D * T + Q * N * T)

F32 = mybir.dt.float32
BF16 = mybir.dt.bfloat16
U32 = mybir.dt.uint32
I32 = mybir.dt.int32
U8 = mybir.dt.uint8
FP8X4 = mybir.dt.float8_e4m3fn_x4
FP4X4 = mybir.dt.float4_e2m1fn_x4
ALU = mybir.AluOpType
ACT = mybir.ActivationFunctionType

P = 128
LOG_AMPLITUDE = 8.4
DIST_SCALE = 128.0


def tile_ardgaussianprocessmean_x2_kernel(
    tc, x, zt, lam, c, alpha_words, alpha_scales, beta_words, beta_scales, out_0, out_1, out_2
):
    nc = tc.nc
    with ExitStack() as ctx:
        keep = ctx.enter_context(tc.tile_pool(name="keep", bufs=1))
        work = ctx.enter_context(tc.tile_pool(name="work", bufs=2))
        psum_t = ctx.enter_context(tc.psum_pool(name="psum_t", bufs=3))
        psum_1 = ctx.enter_context(tc.psum_pool(name="psum_1", bufs=2))
        psum_2 = ctx.enter_context(tc.psum_pool(name="psum_2", bufs=3))
        ctx.enter_context(tc.manual_schedule())

        lam_col = keep.tile([P, 4], BF16)
        nc.scalar.dma_start(out=lam_col[:], in_=lam.rearrange("(p t) -> p t", t=4))
        c_col = keep.tile([P, 2, 4], BF16)
        nc.scalar.dma_start(out=c_col[:], in_=c.rearrange("(g m t) -> m g t", g=2, t=4))

        z_raw = keep.tile([P, 2, 4, D], BF16, align_bytes=64)
        x_raw = keep.tile([P, 8, D], BF16, align_bytes=64)

        def load_z(g, a):
            nc.sync.dma_start(
                out=z_raw[:, g, 2 * a : 2 * a + 2, :],
                in_=zt[512 * g : 512 * g + 512, :].rearrange("(m t) d -> m t d", t=4)[:, 2 * a : 2 * a + 2, :],
            )

        def load_x(i0, n):
            nc.sync.dma_start(
                out=x_raw[:, i0 : i0 + n, :],
                in_=x[128 * i0 : 128 * (i0 + n), :].rearrange("(i m) d -> m i d", m=P),
            )

        load_z(0, 0)
        load_z(0, 1)
        load_x(0, 2)
        load_z(1, 0)
        load_z(1, 1)
        load_x(2, 2)
        load_x(4, 2)
        load_x(6, 2)

        w_scales = keep.tile([P, 3, T], U8, align_bytes=64)
        w_words = keep.tile([P, 3, 2 * T], U8, align_bytes=64)
        nc.sync.dma_start(out=w_words[:, 0, :].bitcast(I32), in_=beta_words[0].bitcast(I32))
        for g in range(2):
            nc.sync.dma_start(out=w_words[:, 1 + g, :].bitcast(I32), in_=alpha_words[g].bitcast(I32))

        zeros = keep.tile([P, 512], BF16)
        nc.vector.memset(zeros[:], 0.0)
        one = keep.tile([P, 1], F32)
        nc.vector.memset(one[:], 1.0)
        warm = keep.tile([P, 2], F32)
        nc.scalar.activation(out=warm[:, 0:1], in_=one[:], func=ACT.Ln)
        ident = keep.tile([P, P], F32)
        make_identity(nc, ident[:])

        nc.vector.memset(w_scales[:].bitcast(I32), 0)
        for k in range(4):
            rows = slice(4 * k, 4 * k + 4)
            parts = slice(32 * k, 32 * k + 4)
            nc.sync.dma_start(
                out=w_scales[parts, 0:1, :].bitcast(I32),
                in_=beta_scales[:, rows, :].rearrange("g q n -> q g n").bitcast(I32),
            )
            nc.sync.dma_start(
                out=w_scales[parts, 1:3, :].bitcast(I32),
                in_=alpha_scales[:, rows, :].rearrange("g q n -> q g n").bitcast(I32),
            )

        lam_f = keep.tile([P, 4], F32)
        nc.vector.tensor_copy(out=lam_f[:], in_=lam_col[:])
        lam_two = keep.tile([P, 4], F32)
        nc.vector.tensor_scalar(out=lam_two[:], in0=lam_col[:], scalar1=2.0, scalar2=None, op0=ALU.mult)
        inv_half = keep.tile([P, 4], F32)
        nc.vector.reciprocal(out=inv_half[:], in_=lam_two[:])
        diag = keep.tile([P, 4, P], BF16)
        halves = keep.tile([P, 4], F32)
        nc.vector.memset(halves[:], 0.5)
        lam_half = keep.tile([P, 4], F32)
        nc.vector.tensor_scalar(out=lam_half[:], in0=lam_col[:], scalar1=0.5, scalar2=None, op0=ALU.mult)
        roots = keep.tile([P, 2, 4], F32)
        diag_2 = keep.tile([P, 2, 2, 4, P], BF16)

        def root_of(w):
            nc.gpsimd.tensor_tensor(out=roots[:, w, :], in0=(inv_half, lam_half)[w][:], in1=halves[:], op=ALU.pow)

        root_of(0)


        def diag_hi(w, t):
            nc.vector.tensor_scalar(
                out=diag_2[:, w, 0, t, :], in0=ident[:], scalar1=roots[:, w, t : t + 1], scalar2=None, op0=ALU.mult
            )

        def diag_lo(w, t):
            nc.vector.scalar_tensor_tensor(
                out=diag_2[:, w, 1, t, :], in0=ident[:], scalar=roots[:, w, t : t + 1], in1=diag_2[:, w, 0, t, :],
                op0=ALU.mult, op1=ALU.subtract,
            )


        def warm_pe(n):
            for r in range(n):
                ps = psum_2.tile([P, 512], F32, tag="ps2", name="ps")
                nc.tensor.matmul(out=ps[:], lhsT=zeros[:, 0:P], rhs=zeros[:], start=True, stop=True)

        def diag_of(t):
            nc.vector.tensor_scalar(out=diag[:, t, :], in0=ident[:], scalar1=lam_f[:, t : t + 1], scalar2=None, op0=ALU.mult)

        c_flat = c_col[:].rearrange("p g t -> p (g t)")
        c_abs = keep.tile([P, 8], F32)
        c_neg = keep.tile([P, 8], BF16)
        c_log = keep.tile([P, 8], F32)
        c_sign = keep.tile([P, 2, 4], BF16)
        c_off = keep.tile([P, 8], F32)

        def c_start():
            nc.vector.scalar_tensor_tensor(out=c_abs[:], in0=c_flat, scalar=-1.0, in1=c_flat, op0=ALU.mult, op1=ALU.max)
            nc.vector.tensor_scalar(out=c_neg[:], in0=c_flat, scalar1=0.0, scalar2=None, op0=ALU.is_lt)
            nc.vector.tensor_scalar_max(out=c_abs[:], in0=c_abs[:], scalar1=1.2e-38)

        def ln_c():
            nc.scalar.activation(out=c_log[:], in_=c_abs[:], func=ACT.Ln)
            nc.scalar.activation(out=warm[:, 1:2], in_=one[:], func=ACT.Exp)

        def c_finish():
            nc.vector.scalar_tensor_tensor(
                out=c_sign[:].rearrange("p g t -> p (g t)"), in0=c_flat, scalar=0.0, in1=c_neg[:], op0=ALU.is_gt, op1=ALU.subtract
            )
            nc.vector.tensor_scalar(
                out=c_off[:], in0=c_log[:], scalar1=DIST_SCALE / 2, scalar2=LOG_AMPLITUDE * DIST_SCALE / 2,
                op0=ALU.mult, op1=ALU.add,
            )

        z_grp = keep.tile([P, N, 4], BF16, align_bytes=64)
        x_grp = keep.tile([P, Q, 4], BF16, align_bytes=64)
        z_codes = keep.tile([P, N], U32, align_bytes=64)
        z_scales = keep.tile([P, N], U8, align_bytes=64)
        x_codes = keep.tile([P, Q], U32, align_bytes=64)
        x_scales = keep.tile([P, Q], U8, align_bytes=64)
        z_bias = keep.tile([P, 8], F32)
        nz_half = keep.tile([P, 8], F32)
        nx_half = keep.tile([P, 8], F32)
        nx_row = keep.tile([P, Q], F32)

        copy_on = {"V": nc.vector.tensor_copy, "S": nc.scalar.copy}
        turned = {}
        scaled = {}

        inv_row = keep.tile([P, D], F32)

        def inv_spread():
            sp = psum_t.tile([P, 4, P], F32, tag="tp", name="sp")
            for t in range(4):
                nc.tensor.transpose(sp[:, t, :], inv_half[:, t : t + 1].to_broadcast([P, P]), ident[:])
            turned["inv"] = sp

        def inv_copy(on):
            copy_on[on](
                out=inv_row[:].rearrange("m (p t) -> m p t", t=4), in_=turned["inv"][:].rearrange("m t p -> m p t")
            )

        def raw_pair(w, k):
            return z_raw[:, k // 2, 2 * (k % 2) : 2 * (k % 2) + 2, :] if w == 0 else x_raw[:, 2 * k : 2 * k + 2, :]

        def turn(w, k):
            tp = psum_t.tile([P, 2, 2, P], F32, tag="tp", name="tp")
            for a in range(2):
                words = raw_pair(w, k)[:, a, :].bitcast(F32)
                for u in range(2):
                    nc.tensor.transpose(tp[:, a, u, :], words[:, u : 256 : 2], ident[:])
            turned[w, k] = tp

        def turn_copy(w, k, on):
            grp = (z_grp, x_grp)[w][:, 256 * k : 256 * k + 256, :]
            copy_on[on](
                out=grp.bitcast(F32).rearrange("p (a r) u -> p a r u", a=2),
                in_=turned[w, k][:].rearrange("p a u r -> p a r u"),
            )

        def quant(w, c0, c1):
            nc.vector.quantize_mx(
                out=(z_codes, x_codes)[w][:, c0:c1].bitcast(FP8X4),
                scales=(z_scales, x_scales)[w][:, c0:c1],
                in_=(z_grp, x_grp)[w][:, c0:c1, :].rearrange("p r t -> p (r t)"),
            )

        def wx(i):
            ps = psum_t.tile([P, 4, P], F32, tag="tp", name="sp")
            for t in range(4):
                nc.tensor.matmul(
                    out=ps[:, t, :], lhsT=x_grp[:, P * i : P * i + P, t], rhs=diag[:, t, :], start=True, stop=True
                )
            turned["wx", i] = ps

        def times_root(w, j):
            ps = psum_t.tile([P, 4, P], F32, tag="tp", name="sp")
            for t in range(4):
                for term in range(2):
                    nc.tensor.matmul(
                        out=ps[:, t, :], lhsT=(z_grp, x_grp)[w][:, P * j : P * j + P, t], rhs=diag_2[:, w, term, t, :],
                        start=(term == 0), stop=(term == 1),
                    )
            turned["root", w, j] = ps

        def root_sum(w, j):
            junk = work.tile([P, D], F32, tag="sjunk", bufs=2)
            nc.scalar.activation(
                out=junk[:], in_=turned["root", w, j][:].rearrange("q t p -> q (t p)"), func=ACT.Square,
                accum_out=(nz_half, nx_half)[w][:, j : j + 1],
            )

        def xsum(i):
            junk = work.tile([P, D], F32, tag="vjunk", bufs=2)
            nc.vector.scalar_tensor_tensor(
                out=junk[:].rearrange("q (p t) -> q p t", t=4), in0=turned["wx", i][:].rearrange("q t p -> q p t"), scalar=0.5,
                in1=x_raw[:, i, :].rearrange("q (p t) -> q p t", t=4),
                op0=ALU.mult, op1=ALU.mult, accum_out=nx_half[:, i : i + 1],
            )

        def square(k):
            y = work.tile([P, 2, D], F32, tag="sq", bufs=2, name="y")
            scaled["sq", k] = y
            nc.scalar.activation(out=y[:], in_=raw_pair(0, k), func=ACT.Square)

        def weigh(k, b):
            junk = work.tile([P, D], F32, tag="vjunk", bufs=2)
            j = 2 * k + b
            nc.vector.scalar_tensor_tensor(
                out=junk[:], in0=scaled["sq", k][:, b, :], scalar=1.0, in1=inv_row[:], op0=ALU.mult, op1=ALU.mult,
                accum_out=nz_half[:, j : j + 1],
            )

        def bias(g):
            gc = slice(4 * g, 4 * g + 4)
            nc.vector.tensor_sub(out=z_bias[:, gc], in0=c_off[:, gc], in1=nz_half[:, gc])

        def spread(k):
            sp = psum_t.tile([P, 2, P], F32, tag="tp", name="sp")
            for b in range(2):
                i = 2 * k + b
                nc.tensor.transpose(sp[:, b, :], nx_half[:, i : i + 1].to_broadcast([P, P]), ident[:])
            turned["spread", k] = sp

        def spread_copy(k, on):
            copy_on[on](out=nx_row[:, 256 * k : 256 * k + 256], in_=turned["spread", k][:].rearrange("p k m -> p (k m)"))

        k_codes = keep.tile([P, 4, 2, 256], U32, align_bytes=64)
        k_scales = keep.tile([P, 4, 2, 256], U8, align_bytes=64)
        args = {}
        exps = {}
        scs = {}

        def score_mm(k, g, tt):
            cols = slice(256 * k, 256 * k + 256)
            ps = psum_1.tile([P, 2, 256], F32, tag="ps1")
            scs[k, g, tt] = ps
            for b in range(2):
                j = 4 * g + 2 * tt + b
                nc.tensor.matmul_mx(
                    out=ps[:, b, :],
                    lhsT=z_codes[:, P * j : P * j + P].bitcast(FP8X4),
                    lhsT_scale=z_scales[:, P * j : P * j + P],
                    rhs=x_codes[:, cols].bitcast(FP8X4),
                    rhs_scale=x_scales[:, cols],
                    start=True,
                    stop=True,
                )

        def score_add(k, g, tt):
            cols = slice(256 * k, 256 * k + 256)
            if (k, g) not in args:
                args[k, g] = work.tile([P, 4, 256], F32, tag="arg", bufs=4, name="arg")
            ps = scs[k, g, tt]
            for b in range(2):
                j = 4 * g + 2 * tt + b
                nc.vector.scalar_tensor_tensor(
                    out=args[k, g][:, 2 * tt + b, :], in0=ps[:, b, :], scalar=z_bias[:, j : j + 1], in1=nx_row[:, cols],
                    op0=ALU.add, op1=ALU.subtract,
                )

        def expo(k, g):
            if k not in exps:
                exps[k] = work.tile([P, 2, 256, 4], BF16, tag="ex", bufs=3, align_bytes=64, name="ex")
            nc.scalar.activation(
                out=exps[k][:, g, :, :].rearrange("p (c i) t -> p c t i", i=4),
                in_=args[k, g][:].rearrange("p t (c i) -> p c t i", i=4), func=ACT.Exp, scale=2.0 / DIST_SCALE
            )

        def sign(k, g):
            ex = exps[k][:, g, :, :]
            nc.vector.tensor_tensor(out=ex, in0=ex, in1=c_sign[:, g : g + 1, :].to_broadcast([P, 256, 4]), op=ALU.mult)

        def k_quant(k):
            nc.vector.quantize_mx(
                out=k_codes[:, k, :, :].rearrange("p g q -> p (g q)").bitcast(FP8X4),
                scales=k_scales[:, k, :, :].rearrange("p g q -> p (g q)"),
                in_=exps[k][:].rearrange("p g q t -> p (g q t)"),
            )

        rs = {}
        stored = {}
        rbs = {}
        ps2s = {}
        tps = {}
        ys = {}

        def product(i, g):
            cols = slice(P * i, P * i + P)
            if i not in rs:
                rs[i] = work.tile([P, T], F32, tag="r", bufs=5, name="r")
                rbs[i] = work.tile([P, 2, 2, P, 2], BF16, tag="rb", bufs=3, align_bytes=64, name="rb")
            ps = psum_2.tile([P, 512], F32, tag="ps2")
            ps2s[i, g] = ps
            kq = slice(P * (i % 2), P * (i % 2) + P)
            for k in range(3):
                nc.tensor.matmul_mx(
                    out=ps[:],
                    lhsT=(x_codes[:, cols] if k == 0 else k_codes[:, i // 2, k - 1, kq]).bitcast(FP8X4),
                    lhsT_scale=x_scales[:, cols] if k == 0 else k_scales[:, i // 2, k - 1, kq],
                    rhs=w_words[:, k, 1024 * g : 1024 * g + 1024].bitcast(FP4X4),
                    rhs_scale=w_scales[:, k, 512 * g : 512 * g + 512],
                    start=(k == 0),
                    stop=(k == 2),
                )

        def r_out(i, g, on):
            copy_on[on](out=rs[i][:, 512 * g : 512 * g + 512], in_=ps2s[i, g][:])
            stored[i] = stored.get(i, 0) + 1
            if stored[i] == 2:
                nc.sync.dma_start(out=out_0[P * i : P * i + P, :], in_=rs[i][:])

        def r_round(i, g, on):
            src = rs[i][:, 512 * g : 512 * g + 512].rearrange("q (p u e) -> q u p e", u=2, e=2)
            if on == "V":
                nc.vector.tensor_copy(out=rbs[i][:, g, :, :, :], in_=src)
            else:
                nc.gpsimd.tensor_scalar(
                    out=rbs[i][:, g, :, :, :], in0=src, scalar1=1.0, scalar2=0.0, op0=ALU.mult, op1=ALU.add
                )

        def r_turn(i):
            tps[i] = psum_t.tile([P, 2, 2, P], F32, tag="tp", name="tp")
            for g in range(2):
                for u in range(2):
                    nc.tensor.transpose(
                        tps[i][:, g, u, :], rbs[i][:, g, u, :, :].rearrange("q p e -> q (p e)").bitcast(F32), ident[:]
                    )

        def y_copy(i, on):
            if i // 2 not in ys:
                ys[i // 2] = work.tile([P, 2, 256, 4], BF16, tag="y_grp", bufs=3, align_bytes=64, name="y_grp")
            a = i % 2
            copy_on[on](
                out=ys[i // 2][:, :, P * a : P * a + P, :].bitcast(F32), in_=tps[i][:].rearrange("p g u r -> p g r u")
            )

        def y_quant(k):
            y_codes = work.tile([P, 2, 256], U32, tag="y_codes", bufs=4, align_bytes=64)
            y_scales = work.tile([P, 2, 256], U8, tag="y_scales", bufs=4, align_bytes=64)
            nc.vector.quantize_mx(
                out=y_codes[:].rearrange("p g r -> p (g r)").bitcast(FP8X4),
                scales=y_scales[:].rearrange("p g r -> p (g r)"),
                in_=ys[k][:].rearrange("p g r t -> p (g r t)"),
            )
            q0 = 256 * k
            nc.sync.dma_start(
                out=out_1[:, :, q0 : q0 + 256, :].rearrange("g p m t -> p g (m t)").bitcast(I32),
                in_=y_codes[:].bitcast(I32),
            )
            for b in range(4):
                nc.sync.dma_start(
                    out=out_2[:, 4 * b : 4 * b + 4, q0 : q0 + 256].rearrange("g q n -> q g n").bitcast(I32),
                    in_=y_scales[32 * b : 32 * b + 4, :, :].bitcast(I32),
                )
        square(0)
        turn(0, 0)
        turn(0, 1)
        square(1)
        turn_copy(0, 0, "V")
        root_of(0)
        diag_of(2)
        diag_of(3)
        diag_hi(0, 0)
        diag_hi(0, 1)
        turn(1, 0)
        c_start()
        turn_copy(0, 1, "S")
        diag_lo(0, 0)
        diag_lo(0, 1)
        diag_of(1)
        diag_hi(0, 3)
        diag_of(0)
        ln_c()
        diag_hi(0, 2)
        quant(0, 0, 512)
        inv_spread()
        diag_lo(0, 2)
        diag_lo(0, 3)
        turn_copy(1, 0, "V")
        turn(0, 2)
        inv_copy("S")
        c_finish()
        quant(1, 0, 256)
        weigh(1, 0)
        wx(0)
        turn_copy(0, 2, "S")
        weigh(1, 1)
        wx(1)
        xsum(0)
        score_mm(0, 0, 0)
        xsum(1)
        score_mm(0, 0, 1)
        weigh(0, 1)
        spread(0)
        turn(0, 3)
        weigh(0, 0)
        spread_copy(0, "S")
        turn(1, 1)
        turn_copy(0, 3, "S")
        bias(0)
        times_root(0, 5)
        score_add(0, 0, 0)
        turn_copy(1, 1, "S")
        times_root(0, 4)
        quant(0, 512, 1024)
        root_sum(0, 5)
        wx(2)
        score_add(0, 0, 1)
        root_sum(0, 4)
        score_mm(0, 1, 0)
        wx(3)
        quant(1, 256, 512)
        expo(0, 0)
        times_root(0, 6)
        xsum(2)
        score_mm(0, 1, 1)
        xsum(3)
        times_root(0, 7)
        root_sum(0, 6)
        sign(0, 0)
        spread(1)
        root_sum(0, 7)
        turn(1, 2)
        spread_copy(1, "S")
        bias(1)
        turn(1, 3)
        turn_copy(1, 2, "S")
        score_add(0, 1, 1)
        turn_copy(1, 3, "S")
        score_add(0, 1, 0)
        wx(5)
        wx(4)
        xsum(5)
        wx(6)
        expo(0, 1)
        score_mm(1, 0, 0)
        xsum(4)
        score_mm(1, 0, 1)
        wx(7)
        score_add(1, 0, 0)
        spread(2)
        score_add(1, 0, 1)
        spread_copy(2, "S")
        score_mm(1, 1, 1)
        sign(0, 1)
        expo(1, 0)
        score_mm(1, 1, 0)
        quant(1, 512, 1024)
        k_quant(0)
        score_add(1, 1, 0)
        product(0, 0)
        score_add(1, 1, 1)
        product(0, 1)
        r_out(0, 0, "S")
        sign(1, 0)
        expo(1, 1)
        xsum(6)
        score_mm(2, 0, 0)
        score_mm(2, 0, 1)
        score_add(2, 0, 0)
        product(1, 0)
        r_out(0, 1, "S")
        sign(1, 1)
        score_mm(2, 1, 0)
        r_out(1, 0, "S")
        product(1, 1)
        score_add(2, 0, 1)
        k_quant(1)
        expo(2, 0)
        score_mm(2, 1, 1)
        score_add(2, 1, 0)
        product(2, 0)
        r_round(0, 0, "V")
        r_out(1, 1, "S")
        score_add(2, 1, 1)
        score_mm(3, 0, 1)
        r_out(2, 0, "S")
        product(2, 1)
        xsum(7)
        expo(2, 1)
        r_round(0, 1, "V")
        score_mm(3, 0, 0)
        sign(2, 0)
        spread(3)
        r_turn(0)
        r_out(2, 1, "S")
        r_round(1, 0, "V")
        product(3, 0)
        r_round(1, 1, "V")
        spread_copy(3, "S")
        sign(2, 1)
        y_copy(0, "S")
        r_turn(1)
        score_add(3, 0, 0)
        r_out(3, 0, "S")
        product(3, 1)
        score_add(3, 0, 1)
        y_copy(1, "S")
        k_quant(2)
        score_mm(3, 1, 1)
        expo(3, 0)
        score_mm(3, 1, 0)
        y_quant(0)
        product(4, 0)
        score_add(3, 1, 0)
        r_out(3, 1, "S")
        product(4, 1)
        r_round(2, 0, "V")
        r_out(4, 0, "S")
        score_add(3, 1, 1)
        product(5, 0)
        r_out(4, 1, "S")
        r_round(2, 1, "V")
        sign(3, 0)
        expo(3, 1)
        r_turn(2)
        r_round(3, 0, "V")
        product(5, 1)
        r_round(3, 1, "V")
        r_round(4, 0, "V")
        y_copy(2, "S")
        sign(3, 1)
        r_turn(3)
        r_out(5, 0, "S")
        r_round(4, 1, "V")
        k_quant(3)
        r_turn(4)
        y_copy(3, "S")
        r_round(5, 0, "V")
        product(6, 0)
        y_copy(4, "S")
        y_quant(1)
        r_out(5, 1, "S")
        product(6, 1)
        r_out(6, 0, "S")
        r_round(5, 1, "V")
        r_turn(5)
        r_round(6, 0, "V")
        r_out(6, 1, "S")
        product(7, 0)
        y_copy(5, "S")
        r_round(6, 1, "V")
        product(7, 1)
        y_quant(2)
        r_out(7, 0, "S")
        r_turn(6)
        r_round(7, 0, "V")
        r_out(7, 1, "S")
        y_copy(6, "S")
        r_round(7, 1, "V")
        r_turn(7)
        y_copy(7, "S")
        y_quant(3)
